import numpy as np, ml_dtypes
CORES = [16,17,18,19,32,33,34,35]
N = 8
import mx_ref
BF = ml_dtypes.bfloat16
def gentries(a):
    return np.ascontiguousarray(a.reshape(8, 16, -1).transpose(0, 2, 1)).reshape(8, -1)
def gtable(e):
    e = np.asarray(e); return np.ascontiguousarray(e.reshape(8, -1, 16).transpose(0, 2, 1)).reshape(128, -1).astype(np.int32)
def gcols(t, e):
    v = np.concatenate([t.reshape(8, 16, -1, 4), np.zeros((8, 16, 1, 4), BF)], axis=2)
    return np.ascontiguousarray(np.stack([v[g][:, e[g]] for g in range(8)])).reshape(128, -1)
def tile(rs):
    return np.stack(rs, axis=2).reshape(128, -1).astype(BF)
def pick(q, e):
    c = np.concatenate([q[0].reshape(128, -1, 4), np.zeros((128, 1, 4), np.uint8)], axis=1); s = np.concatenate([q[1], np.ones((16, 1), np.uint8)], axis=1)
    return (np.ascontiguousarray(c[:, e].reshape(128, -1)), np.ascontiguousarray(s[:, e]))
def join(*qs):
    return (np.concatenate([q[0] for q in qs], axis=1), np.concatenate([q[1] for q in qs], axis=1))
def put(q, e, v):
    c, s = q[0].reshape(128, -1, 4).copy(), q[1].copy(); c[:, e] = v[0].reshape(128, -1, 4); s[:, e] = v[1]
    return (c.reshape(128, -1), s)
def pk(c, s):
    return (np.ascontiguousarray(c), mx_ref.live(s))
def emit(q):
    return q[0], q[1]
def packed(v, rng):
    q = [mx_ref.quantize(np.ascontiguousarray(v[r])) for r in range(N)]
    return np.stack([a for a, b in q]), np.stack([mx_ref.plane(b, rng) for a, b in q])
def values_of_codes():
    e, c = np.zeros((128, 128, 4), np.float32), np.zeros((128, 2, 4), np.uint8)
    e[np.arange(128), np.arange(128), 0] = 1
    c[:127, :, 0] = np.arange(256).reshape(2, 128).T[:127]
    return mx_ref.matmul(mx_ref.quantize(e.reshape(128, 512).astype(BF)), (c.reshape(128, 8), np.full((16, 2), 127, np.uint8))).T.reshape(-1).astype(np.float64)
CODE_VALUE, SCALE_VALUE = values_of_codes(), 2.0 ** (np.arange(256) - 127.0)
def decode(q):
    return (CODE_VALUE[q[0]].reshape(16, 8, -1, 4) * SCALE_VALUE[q[1]][:, None, :, None] + 0.0).reshape(128, -1).astype(np.float32)
def f(rng, *shape):
    return mx_ref.flush((rng.standard_normal(shape, dtype=np.float32) * np.exp2(rng.integers(-2, 3, shape[:-1] + (1,)))).astype(BF))
def wide(rng, *shape, cols=0):
    v = rng.standard_normal(shape, dtype=np.float32) * np.exp2(rng.integers(-12, 13, shape)).astype(np.float32)
    if cols: v *= np.repeat(np.exp2(rng.integers(-cols, cols + 1, shape[:-2] + (1, shape[-1] // 4))) * (rng.random(shape[:-2] + (1, shape[-1] // 4)) > 0.0625), 4, axis=-1).astype(np.float32)
    return mx_ref.flush(v.astype(BF))
C, H, E, R = 256, 128, 384, 3
def big(v):
    v = v.astype(np.float32)
    v[np.abs(v) < np.float32(2.0 ** -16)] = 0
    return v.astype(BF)
def numbers_of(rng):
    return {"x": big(f(rng, N, 128, 4 * C)), "u": np.array(f(rng, N, 128, 512)), "v": np.array(f(rng, N, 128, 512))}
def stored(a):
    return np.stack([gtable(a[r]) for r in range(N)])
def lists(rng):
    return {"lf": stored(rng.integers(0, E, (N, 8, E))), "rt": stored(rng.integers(0, E, (N, 8, E)))}
def layers(rng, still=[]):
    w = big(f(rng, N, 128, 2048)).reshape(N, 8, 16, 4, 8, 16, 4)
    for i in still:
        w[:, :, i] = 0
        w[:, :, :, :, :, i] = 0
    return w
def weights(rng, w):
    c, p = packed(np.ascontiguousarray(w).reshape(N, 128, 2048), rng)
    return {"wc": c, "ws": p}
def setup_inputs(rng):
    return {**numbers_of(rng), **lists(rng), **weights(rng, layers(rng))}
def setup_inputs_ties(rng):
    d = numbers_of(rng)
    o = rng.permutation(N)
    x = d["x"].reshape(N, 8, 16, C, 4)
    x[:, :, 0] = 0
    x[:, :, 0, :, 0] = rng.integers(-2, 3, (N, 8, C)).astype(np.float32).astype(BF)
    u = d["u"].reshape(N, 128, 128, 4)
    u[:, :, ::16] = 0
    for h in range(0, 128, 16): u[:, h, h, 0] = 1
    u[o[0], :, ::16] = 0
    e = lists(rng)
    e["rt"][o[1]] = e["lf"][o[1]]
    return {"x": x.reshape(N, 128, 4 * C), "u": u.reshape(N, 128, 512), "v": d["v"], **e, **weights(rng, layers(rng, [0]))}
def setup_inputs_near(rng):
    d = numbers_of(rng)
    kind = rng.permutation(8) % 4
    x = d["x"].astype(np.float32).reshape(N, 8, 16, C, 4)
    c = rng.integers(0, 2, (N, 8, C)) * 2.0 - 1.0
    s = rng.integers(0, 16, (N, 8, C))
    x[:, :, 0] = 0
    x[:, :, 8:] = 0
    x[:, :, 0, :, 0] = c
    x[:, :, 8] = c[:, :, :, None] * ((s[:, :, :, None] >> np.arange(4)) & 1) * np.exp2(np.arange(4) - 23.0)
    x[:, :, 11, :, 0] = c * 2.0 ** -10
    u = d["u"].reshape(N, 128, 128, 4)
    u[:, :, ::16] = 0
    for g in range(8):
        h, m = 16 * g, 1.0 if kind[g] == 0 else 2.0 ** -30
        if kind[g] < 2:
            u[:, h, h, 0] = m
            u[:, h + 11, h, 0] = m
        if kind[g] < 3: u[:, h + 8, h] = m
        else:
            a = rng.integers(0, 2, (N, C))
            x[:, g, 8:] = 0
            x[:, g, 10, :, 0] = c[:, g] * a * 1.125 * 2.0 ** -30
            x[:, g, 10, :, 1] = c[:, g] * (1 - a) * 1.25 * 2.0 ** -30
            u[:, h + 10, h, 0] = m * 1.125
            u[:, h + 10, h, 1] = m
    x = (x + np.float32(0.0)).reshape(N, 128, 4 * C).astype(BF)
    return {"x": x, "u": u.reshape(N, 128, 512), "v": d["v"], **lists(rng), **weights(rng, layers(rng, [0, 8, 9, 10, 11, 12, 13, 14, 15]))}
def setup_inputs_twice(rng):
    d = numbers_of(rng)
    x = (2 * rng.integers(0, 8, (N, 8, 16, C, 4)) + 1) * np.exp2(rng.integers(-17, -15, (N, 8, 16, C, 4))) * (rng.integers(0, 2, (N, 8, 16, C, 4)) * 2.0 - 1.0)
    x[:, :, ::8, :, 0] = np.where(rng.random((N, 8, 2, C)) < 0.5, 1.96875, 1.75) * (rng.integers(0, 2, (N, 8, 2, C)) * 2.0 - 1.0)
    a = int(rng.integers(1, 8))
    x[:, a, ::8, :, 0] = 1.75
    t = np.arange(C) % 4 == rng.integers(0, 4, (N, 1))
    x[:, 0] = np.where(t[:, None, :, None], 0.0, x[:, 0])
    x[:, 0, ::8, :, 0] = np.where(t[:, None], 1.75 * 2.0 ** -24 * (rng.integers(0, 2, (N, 2, C)) * 2.0 - 1.0), x[:, 0, ::8, :, 0])
    u = d["u"].reshape(N, 128, 128, 4)
    u[:, ::8, ::16] = 0
    w = np.zeros((N, 128, 4, 128, 4), np.float32)
    i = np.arange(128)
    for b in range(4): w[:, i, b, i, b] = -32
    w[:, i[::16], 0, i[::16], 0] = -36
    w[:, i[8::16], 0, i[8::16], 0] = -18
    w[:, :, :, :16] = 0
    w[:, :, :, 16 * a:16 * a + 16] = 0
    m = np.arange(16)
    k = np.where(np.arange(N) % 2 == rng.integers(0, 2), 1.0, -1.0)[:, None]
    for b in range(4): w[:, 16 * a + m, b, m, b] = 32 * k
    w[:, 16 * a + m[::8], 0, m[::8], 0] = 36 * k
    e = rng.integers(0, E, (2, N, 8, E))
    for r in range(N):
        e[:, r, 0, :C] = rng.permutation(np.concatenate([np.arange(H), np.arange(C, E), H + rng.permutation(C - H)[:C - 2 * H]]))
    return {"x": x.astype(np.float32).reshape(N, 128, 4 * C).astype(BF), "u": u.reshape(N, 128, 512), "v": d["v"], "lf": stored(e[0]), "rt": stored(e[1]), **weights(rng, w.astype(BF))}
def setup_inputs_ends(rng):
    d = numbers_of(rng)
    e = rng.permutation(N)
    h = rng.permutation(8)
    most = 1.34375 * 2.0 ** 28
    x = (0.6 + 0.4 * rng.random((N, 8, 16, C, 4))) * most
    x[e[::2]] = most
    c = rng.integers(0, 2, (N, 1, 1, C, 1)) * 2.0 - 1.0
    c[e[1]] = c[e[1], 0, 0, 0, 0]
    x = x * c
    x[:, h[4:], 8:] = (rng.integers(0, 2, (N, 4, 8, C, 4)) * 2.0 - 1.0) * 2.0 ** -30
    u = d["u"].reshape(N, 128, 128, 4)
    u[:, :, ::16] = 0
    for g in h[:4]: u[:, :, 16 * g] = (2.0 ** 30 * (1.0 - 0.1 * rng.random((N, 128, 4))) * rng.choice([-1.0, 1.0], (N, 1, 1))).astype(np.float32).astype(BF)
    for g in h[4:]: u[:, 16 * g + 8:16 * g + 16, 16 * g] = 2.0 ** -30
    u[e[2], :, ::16] = 0
    v = d["v"]
    v[e[:2]] = (2.0 ** 30 * rng.choice([-1.0, 1.0], (2, 128, 512))).astype(np.float32).astype(BF)
    a = rng.integers(0, 2, (2, N, 8, E)) * (E - 1)
    a[:, e[0]] = E - 1
    a[:, e[1]] = 0
    a[:, e[2]] = np.argsort(rng.random((2, 8, E)), axis=2)
    p, m = np.arange(C), rng.permutation(C)
    for g, k in enumerate(rng.permutation(8)):
        t = rng.permutation(E)
        if k == 0: t = np.concatenate([rng.permutation(C), C + rng.permutation(H)])
        elif H * (k - 1) < C: t = np.concatenate([C + rng.permutation(H), rng.permutation(C)])
        a[0, e[2], g, np.concatenate([p[np.roll(m, -H * (k - 1))], np.setdiff1d(np.arange(E), p)])] = t
        p = a[0, e[2], g, p]
    a[:, e[3]] = rng.integers(0, C, (2, 8, E))
    w = np.zeros((N, 128, 4, 128, 4), np.float32)
    i = np.flatnonzero(np.arange(128) % 16 < 8)
    k = rng.choice([-4.0, 4.0], (N, 1))
    for b in range(4): w[:, i, b, i, b] = k
    v = (np.where(v < 0, -1.0, 1.0) * np.where(rng.permutation(N) % 2, 2.0 ** -30, 2.0 ** 30)[:, None, None]).astype(np.float32).astype(BF)
    return {"x": x.astype(np.float32).reshape(N, 128, 4 * C).astype(BF), "u": u.reshape(N, 128, 512), "v": v, "lf": stored(a[0]), "rt": stored(a[1]), **weights(rng, w.astype(BF))}
def setup_inputs_spread(rng):
    d = numbers_of(rng)
    w = (layers(rng).astype(np.float32) * np.float32(0.125)).astype(BF)
    return {"x": big(wide(rng, N, 128, 4 * C, cols=4)), "u": d["u"], "v": d["v"], **lists(rng), **weights(rng, w)}
def check_inputs(d):
    b = []
    for k in ("x", "u", "v"):
        a = np.abs(d[k].astype(np.float32))
        if not (np.isfinite(a).all() and ((a == 0) | (a >= 2.0 ** -30) & (a <= 2.0 ** 30)).all()): b.append("a value of " + k)
    for k in ("lf", "rt"):
        if not ((d[k] >= 0) & (d[k] < E)).all(): b.append("an entry of " + k)
    none, least, most = [emit(mx_ref.quantize(np.full((128, 16), k, np.float32).astype(BF)))[1][0, 0] for k in (0.0, 2.0 ** -30, 2.0 ** 30)]
    size = 0.0
    for r in range(N):
        if ((d["wc"][r] == 0x7F) | (d["wc"][r] == 0xFF)).any(): b.append("wc: a code that is no number")
        s = mx_ref.live(d["ws"][r])
        if ((s != none) & ((s < least) | (s > most))).any(): b.append("ws: a scale out of range")
        full = ((d["wc"][r] & 0x7F) != 0).reshape(16, 8, 512, 4).any(axis=(1, 3))
        if (full & (s == none)).any(): b.append("wc: a code other than zero at the scale of zeros")
        with np.errstate(all="ignore"):
            size = np.maximum(size, np.max(np.sum(np.abs(decode(pk(d["wc"][r], d["ws"][r])).astype(np.float64)).reshape(128, 512, 4), axis=(0, 2))))
    with np.errstate(all="ignore"):
        if not np.max(np.abs(d["x"].astype(np.float64))) * (1.125 + 2.5 * size * 2.0 ** -5) ** 3 <= 2.0 ** 30: b.append("the sizes of x and W together")
    return b
def reference(x, u, v, lf, rt, wc, ws):
    qu = [mx_ref.quantize(u[r]) for r in range(N)]
    lay = [pk(wc[r], ws[r]) for r in range(N)]
    left = [gentries(lf[r]) for r in range(N)]
    right = [gentries(rt[r]) for r in range(N)]
    now = [x[r] for r in range(N)]
    took = np.zeros((N, 8, C), np.int64)
    for t in range(R):
        q = [mx_ref.quantize(now[r]) for r in range(N)]
        edge = [pick(q[r], np.arange(H)) for r in range(N)]
        own = [decode(q[r]) for r in range(N)]
        flux, back = [], []
        for r in range(N):
            e = (r + 1) % N
            s = np.abs(mx_ref.matmul(qu[r], join(q[r], edge[e]))[::16])
            l, k = np.arange(C), np.arange(C)
            for g in range(8):
                a, b = left[r][g, l], right[r][g, k]
                first = s[g, a] <= s[g, b]
                took[r, g] = np.where(first, a, b)
                l, k = np.where(first, a, l), np.where(first, k, b)
            window = np.concatenate([own[r], own[e][:, :4 * H]], axis=1).astype(BF)
            z = mx_ref.quantize(gcols(window, took[r]))
            h = mx_ref.quantize(tile([mx_ref.matmul(pick(lay[r], np.arange(128 * b, 128 * b + 128)), z) * np.float32(0.03125) for b in range(4)]))
            c = np.full((8, E), -1)
            for g in range(8):
                i, j = np.unique(took[r, g], return_index=True)
                c[g, i] = j
            w = gcols(decode(h).astype(BF), c)
            flux.append(w[:, :4 * C].astype(np.float32))
            back.append(decode(mx_ref.quantize(np.ascontiguousarray(w[:, 4 * C:]))))
        for r in range(N):
            n = own[r] - flux[r]
            n[:, :4 * H] = n[:, :4 * H] - back[(r - 1) % N]
            now[r] = n.astype(BF)
    y, on = np.zeros((N, 128, C), np.float32), np.zeros((N, 8, C), np.float32)
    oc, osc = np.zeros((N, 128, 4 * C), np.uint8), np.zeros((N, 16, C), np.uint8)
    for r in range(N):
        q = mx_ref.quantize(now[r])
        y[r] = mx_ref.matmul(mx_ref.quantize(v[r]), q)
        on[r] = took[r]
        oc[r], osc[r] = emit(q)
    return {"y": y, "on": on, "oc": oc, "osc": osc}

@@ -1,0 +1,437 @@
+from concourse.mybir import dt, AluOpType, ActivationFunctionType
+
+OP = AluOpType
+AF = ActivationFunctionType
+N, R, C, H, E = 8, 3, 256, 128, 384
+CW = 816
+PW = 272
+EARLY = 4
+PRE = 2
+LISTS = ("float8_e4m3fn_x4 QX 384 QU 128 UQ 1024 QV 128 WQ 512 QE 512 QM 256 QT 256 QB 128 LB 128",
+         "uint8 SX 384 SU 128 US 1024 SV 128 WS 512 SE 512 SM 256 SQ 256 SB 128 LS 128",
+         "bfloat16 X 1024 UIN 512 VIN 512 ONES 512 EB 2048 VP 1536 M 1024 TT 1024 DW 1088 CELL0 816 CELL1 816 "
+         "CELL2 816 CELL3 816 CELL4 816 CELL5 816 POS 256 CT0 768 CT1 768 UB 512",
+         "float32 IOTA 768 TAB 6144 SCP 3456 PQ 64 SCN 1024 CS 256 GT 128 GB 32 GA 32 D1 32 D2 32 BU 16 AB 16 FA 16 NB 16 "
+         "UNW 256 CEA 16 EE 512 DS 512 FLB 16 MXB 16 CM 24 CA 24 CB 24 FU 512 MASK 128 MINM 32 RM 128 CDG 512 PF 8 YO 256 ONR 256",
+         "int32 LST 384 NI 16 T1 16 MD 128 MDA 128 ME 512 MF 512 MI 128 MJ 128 PI 8 UOI 64 RI 32",
+         "uint16 LSU 384 OF 64 NU 16 OFN 16 OFS 16 OFC 24 UOF 64 REP 32 REV 16")
+WIDTH = {}
+SCRATCH = {}
+for _line in LISTS:
+    _w = _line.split()
+    for _i in range(1, len(_w), 2):
+        WIDTH[_w[_i]] = int(_w[_i + 1])
+        SCRATCH[_w[_i]] = ("sbuf", [128, int(_w[_i + 1])], _w[0])
+for _i in range(8):
+    WIDTH["ps%d" % _i] = 512
+    SCRATCH["ps%d" % _i] = ("psum", [128, 512], "float32")
+SEMAPHORES = ["v", "s", "pe", "gp", "lx0", "lx1", "lu", "lv", "lwc", "lws", "la", "lb", "lr", "exa", "ex4", "ex5", "ex6",
+              "ex7", "outs", "oute", "brd", "bar", "sbrd", "sbar"]
+
+
+def rank_program(g, core, T, topo):
+    rank = T.rank_of(core)
+    if rank is None:
+        return
+    nxt, prv = T.cores[(rank + 1) % N], T.cores[(rank - 1) % N]
+    v, s = g.vector, g.scalar
+    eng = {"pe": g.tensor, "v": v, "s": s, "g": g, "y": g.sync}
+    home = {"pe": "pe", "v": "v", "s": "s", "g": "gp"}
+    count = {k: 0 for k in SEMAPHORES}
+    held = {}
+    log = {}
+
+    def B(n, a=0, b=None, st=1, ix=None, bit=None, p=(0, 128)):
+        b = WIDTH[n] if b is None else b
+        ap = T[n][p[0]:p[1], a:b] if st == 1 else T[n][p[0]:p[1], a:b:st]
+        if bit:
+            ap = ap.bitcast(bit)
+        if ix:
+            ap = ap.indirect(ix[0])
+        return (ap, [(n, p[0], p[1], a, b, st)], ix[1] if ix else [])
+
+    def wait(q, sem, val):
+        if held.get((q, sem), 0) < val:
+            held[(q, sem)] = val
+            eng[q].wait_ge(T.sem[sem], val)
+
+    def order(q, reads, writes):
+        need = {}
+        for kinds, regs in (("wW", reads), ("rw", writes)):
+            for n, p0, p1, c0, c1, st in regs:
+                for k, a0, a1, b0, b1, su, sem, val, far in log.get(n, ()):
+                    if k in kinds and a0 < p1 and p0 < a1 and b0 < c1 and c0 < b1 and (st != su or (c0 - b0) % st == 0):
+                        need[sem] = max(need.get(sem, 0), count[sem] if far else val)
+        for sem in need:
+            wait(q, sem, need[sem])
+
+    def note(reads, writes, sem, far):
+        for n, p0, p1, c0, c1, st in writes:
+            log[n] = [x for x in log.get(n, ()) if not (p0 <= x[1] and x[2] <= p1 and c0 <= x[3] and x[4] <= c1
+                                                        and (st == 1 or st == x[5] and (c0 - x[3]) % st == 0))]
+        for n, p0, p1, c0, c1, st in reads:
+            if st == 1:
+                log[n] = [("W",) + x[1:] if x[0] == "w" and p0 <= x[1] and x[2] <= p1 and c0 <= x[3] and x[4] <= c1 else x
+                          for x in log.get(n, ())]
+        for kind, regs in (("w", writes), ("r", reads)):
+            for r in regs:
+                log.setdefault(r[0], []).append((kind,) + r[1:] + (sem, count[sem], far))
+
+    def run(q, call, *args, outs=1, **kw):
+        reads, writes, real = [], [], []
+        for i, x in enumerate(args):
+            if isinstance(x, tuple):
+                (writes if i < outs else reads).extend(x[1])
+                reads.extend(x[2])
+                x = x[0]
+            real.append(x)
+        order(q, reads, writes)
+        call(*real, **kw).then_inc(T.sem[home[q]], 1)
+        count[home[q]] += 1
+        note(reads, writes, home[q], False)
+
+    def dma(q, sem, out, in_):
+        w, r = (out[1] if isinstance(out, tuple) else []), (in_[1] if isinstance(in_, tuple) else [])
+        order(q, r, w)
+        eng[q].dma_start(out[0] if isinstance(out, tuple) else out, in_[0] if isinstance(in_, tuple) else in_).then_inc(T.sem[sem], 16)
+        count[sem] += 16
+        note(r, w, sem, True)
+
+    def engines(a, b):
+        return topo.engines(a, b)[:8]
+
+    def exchange(dst, src, pairs, remote, local):
+        reads = [r for o, i in pairs for r in i[1]]
+        order("g", reads, [])
+        rid, pid, _ = topo.addr(dst)
+        es = engines(core, dst)
+        for o, i in pairs:
+            g.remote_dma(out_ap=o[0], in_ap=i[0], remote_sem=T.sem[remote], local_sem=T.sem[local], pid=pid, routing_id=rid,
+                         dma_engine_mask=sum(1 << e for e in es))
+            count[local] += len(es)
+        note(reads, [], local, True)
+        count[remote] += len(pairs) * len(engines(src, core))
+        note([], [r for o, i in pairs for r in o[1]], remote, True)
+
+    def ts(out, in0, s1, op0, s2=None, op1=None):
+        run("v", v.tensor_scalar, out, in0, s1, s2, op0, *((op1,) if op1 else ()))
+
+    def tt(out, in0, in1, op):
+        run("v", v.tensor_tensor, out, in0, in1, op)
+
+    def cp(out, in_):
+        run("v", v.tensor_copy, out, in_)
+
+    def act(out, in_, func=AF.Copy, **kw):
+        run("s", s.activation, out, in_, func, **kw)
+
+    def scan(out, d0, d1, op0, op1):
+        run("v", v.tensor_tensor_scan, out, d0, d1, 0.0, op0, op1)
+
+    def fill(x, c):
+        run("v", v.memset, x, c)
+
+    def iota(out, step, n, base, cm):
+        run("g", g.iota, out, [[step, n]], base, cm, allow_small_or_imprecise_dtypes=True)
+
+    def quant(q, sc, a, b, tile):
+        run("v", v.quantize_mx, B(q, a, b), B(sc, a, b), B(tile, 4 * a, 4 * b), outs=2)
+
+    bank = [0]
+
+    def mm(lq, ls, la, rq, rs, a, b):
+        p = "ps%d" % (bank[0] % 8)
+        bank[0] += 1
+        run("pe", g.tensor.matmul_mx, B(p, 0, b - a), B(lq, la, la + 128), B(ls, la, la + 128), B(rq, a, b), B(rs, a, b), True, True)
+        return B(p, 0, b - a)
+
+    def score(k, a, b):
+        o = E * (k + 1)
+        act(B("SCP", o + a, o + b), mm("UQ", "US", 128 * k, "QX", "SX", a, b), AF.Abs)
+
+    def send_border():
+        exchange(prv, nxt, ((B("QX", C, E, bit=dt.uint8), B("QX", 0, H, bit=dt.uint8)), (B("SX", C, E), B("SX", 0, H))), "brd", "sbrd")
+
+    soon, todo = [], []
+
+    def spare():
+        if soon:
+            soon.pop(0)()
+
+    def later(f, *a, to=todo):
+        to.append(lambda: f(*a))
+
+    dma("y", "lx0", B("X", 0, 512), T.x[:, 0:512])
+    dma("s", "lu", B("UIN"), T.u[:])
+    for k in range(8):
+        dma("y", "la", B("LST", 48 * k, 48 * k + 24, p=(0, 16)), T.lf[16 * k:16 * k + 16, :])
+        dma("s", "lb", B("LST", 48 * k + 24, 48 * k + 48, p=(0, 16)), T.rt[16 * k:16 * k + 16, :])
+    dma("y", "lx1", B("X", 512, 1024), T.x[:, 512:1024])
+    for h in range(1, 8):
+        dma("y", "lr", B("LST", p=(16 * h, 16 * h + 16)), B("LST", p=(0, 16)))
+    iota(B("IOTA", 0, E), 1, E, 0, 0)
+    iota(B("PI", 0, 1), 1, 1, 0, 1)
+    iota(B("IOTA", E, 2 * E), 1, E, E, 0)
+    fill(B("ONES"), 1.0)
+    cp(B("MI"), B("IOTA", 0, 128))
+    ts(B("UOI"), B("MI", 0, 64), 0x38, OP.bitwise_and)
+    ts(B("UOF"), B("UOI"), 2, OP.mult)
+    cp(B("PF", 0, 1), B("PI", 0, 1))
+    quant("QX", "SX", 0, H, "X")
+    send_border()
+    iota(B("SCP", 0, E), 1, E, 0, 0)
+    for b in range(4):
+        run("g", g.affine_select, B("EB", 512 * b, 512 * b + 512), B("ONES"), [[-8, 128], [-1, 4]], OP.is_equal, 0.0, b, 8)
+    iota(B("POS"), 1, 256, 1, 0)
+    for x in range(2 * R):
+        iota(B("CELL%d" % x), 0, CW, 0, 0)
+    dma("s", "lwc", B("WQ", bit=dt.uint8), T.wc[:])
+    dma("s", "lws", B("WS"), T.ws[:])
+    dma("y", "lv", B("VIN"), T.v[:])
+    quant("QU", "SU", 0, 128, "UIN")
+    cp(B("UQ", bit=dt.uint32), B("QU", bit=dt.uint32, ix=B("UOF")))
+    act(B("US"), B("SU", ix=B("UOF")))
+    quant("QX", "SX", H, C, "X")
+    for k in range(8):
+        score(k, 0, C)
+    ts(B("MD"), B("IOTA", 0, 128), B("PF", 0, 1), OP.subtract, 256.0, OP.add)
+    ts(B("PI", 1, 2), B("PI", 0, 1), 7, OP.bitwise_and)
+    ts(B("PI", 2, 3), B("PI", 0, 1), 3, OP.arith_shift_right)
+    ts(B("MDA"), B("MD"), 15, OP.bitwise_and)
+    ts(B("PF", 5, 6), B("PI", 1, 2), 32, OP.mult)
+    ts(B("MJ"), B("MI"), 15, OP.bitwise_and)
+    ts(B("MASK"), B("MDA"), 0, OP.is_equal)
+    tt(B("PF", 1, 2), B("PF", 5, 6), B("PI", 2, 3), OP.add)
+    ts(B("RM"), B("MJ"), 0, OP.not_equal)
+    ts(B("MINM"), B("MASK", 0, 32), 1e29, OP.mult, -1.0, OP.add)
+    for x in range(4):
+        ts(B("OF", 2 + x, 3 + x), B("PF", 1, 2), -1.0, OP.mult, float(255 - 16 * (x % 2) + E * (1 - x // 2)), OP.add)
+    cp(B("LSU"), B("LST"))
+
+    def table(q, k):
+        for x in range(2):
+            o, l = 768 * k + E * x, 48 * k + 24 * x
+            (cp if q == "v" else act)(B("TAB", o, o + E), B("IOTA", E * x, E * x + E, ix=B("LSU", l, l + 24)))
+
+    def col(buf, x):
+        return B(buf, x, x + 1)
+
+    def candidates(k):
+        tt(B("GT"), B("TAB", 768 * k + 768, 768 * k + 1536, ix=B("OF", 8 * k, 8 * k + 8)), B("MASK"), OP.mult)
+
+    def candidates_own(k):
+        scan(B("SCN", 128 * k, 128 * k + 128), B("RM"), B("GT"), OP.mult, OP.add)
+
+    def diff_ends(k):
+        tt(B("D2", 4 * k, 4 * k + 4), B("PQ", 8 * k, 8 * k + 4), B("PQ", 8 * k + 4, 8 * k + 8), OP.subtract)
+
+    def diff_candidates(k):
+        tt(B("D1", 4 * k, 4 * k + 4), B("SCN", 128 * k + 15, 128 * k + 64, 16), B("SCN", 128 * k + 79, 128 * k + 128, 16), OP.subtract)
+
+    table("v", 0)
+    tt(B("GT", 0, 64), B("TAB", 0, 768, ix=B("OF", 2, 6)), B("MASK", 0, 64), OP.mult)
+    scan(B("SCN", 0, 64), B("RM", 0, 64), B("GT", 0, 64), OP.mult, OP.add)
+    cp(B("OF", 6, 8), B("SCN", 15, 32, 16))
+    cp(B("OF", 0, 2), B("SCN", 47, 64, 16))
+    table("v", 1)
+    cp(B("PQ", 0, 8), B("OF", 0, 8))
+    candidates(0)
+    diff_ends(0)
+    candidates_own(0)
+    diff_candidates(0)
+    later(ts, B("PI", 3, 4), B("PI", 0, 1), 15, OP.bitwise_and)
+    later(ts, B("PI", 4, 5), B("PI", 0, 1), 16, OP.bitwise_and)
+    for x in range(2):
+        later(ts, B("RI", 16 * x, 16 * x + 16), B("MI", 0, 16), 14, OP.bitwise_and)
+    later(cp, B("PF", 4, 5), B("PI", 3, 4))
+    later(cp, B("PF", 3, 4), B("PI", 4, 5))
+    later(ts, B("PF", 2, 3), B("PI", 3, 4), 768, OP.add)
+    later(ts, B("PF", 6, 7), B("PI", 3, 4), 784, OP.add)
+    for x in range(2):
+        later(ts, B("ME", 256 * x, 256 * x + 256), B("IOTA", 0, 256), B("PF", 4, 5), OP.subtract, 256.0 - 16 * x, OP.add)
+        later(ts, B("REP", 16 * x, 16 * x + 16), B("RI", 16 * x, 16 * x + 16), x, OP.add)
+    later(ts, B("PF", 7, 8), B("PF", 4, 5), -1.0, OP.mult, 255.0, OP.add)
+    later(ts, B("MF"), B("ME"), 31, OP.bitwise_and)
+    later(quant, "QV", "SV", 0, 128, "VIN")
+    for b in range(4):
+        later(fill, B("DW", PW * b, PW * b + 1), 0.0)
+    later(ts, B("CDG"), B("MF"), 0, OP.not_equal)
+    later(ts, B("REV"), B("IOTA", 0, 16), -16.0, OP.mult, B("PF", 7, 8), OP.add)
+
+    def list_out(k, sem):
+        dma("y", sem, B("OFN", p=(16 * k, 16 * k + 16)), B("NU", 2 * k, 2 * k + 2))
+
+    def lists_out(k0, k1, sem):
+        def part(buf, j):
+            return B(buf, 2 * k0 + j, 2 * k1, 2)
+
+        def end():
+            cp(B("NU", 2 * k0, 2 * k1), B("NB", 2 * k0, 2 * k1))
+            for k in range(k0, k1):
+                list_out(k, sem)
+
+        for j in range(2):
+            later(ts, part("BU", j), B("PQ", 8 * k0 + 6 + j, 8 * k1, 8), -float(E), OP.add, to=soon)
+        for j in range(2):
+            later(tt, part("AB", j), B("PQ", 8 * k0 + j, 8 * k1, 8), part("BU", j), OP.subtract, to=soon)
+        for j in range(2):
+            later(tt, part("FA", j), B("CS", 32 * k0 + 15 + 16 * j, 32 * k1, 32), part("AB", j), OP.mult, to=soon)
+        for j in range(2):
+            later(tt, part("NB", j), part("FA", j), part("BU", j), OP.add, to=soon)
+        later(end, to=soon)
+
+    def right_place(k):
+        ts(B("BU", 2 * k, 2 * k + 2), B("PQ", 8 * k + 6, 8 * k + 8), -float(E), OP.add)
+
+    def place_diff(k):
+        tt(B("AB", 2 * k, 2 * k + 2), B("PQ", 8 * k, 8 * k + 2), B("BU", 2 * k, 2 * k + 2), OP.subtract)
+
+    def places(k):
+        for j in range(2):
+            ts(col("NU", 2 * k + j), col("CS", 32 * k + 15 + 16 * j), col("AB", 2 * k + j), OP.mult, col("BU", 2 * k + j), OP.add)
+        list_out(k, "ex%d" % k)
+
+    for t in range(R):
+        last = t == R - 1
+
+        def numbers():
+            for b in range(4):
+                act(B("VP", E * b, E * b + E), mm("QE", "SE", 128 * b, "QX", "SX", 0, E))
+
+        if t == 0:
+            table("s", 2)
+        for k in range(8):
+            score(k, C, E)
+            if t == 0 and 1 <= k < 6:
+                table("s", k + 2)
+        if t:
+            numbers()
+        for k in range(8):
+            if t == 0 and k == 3:
+                quant("QE", "SE", 0, 512, "EB")
+                numbers()
+            o, c, n = E * k, 32 * k, 8 * k
+            tt(B("GB"), B("SCP", o, o + 2 * E, ix=B("OF", n + 6, n + 8)), B("MINM"), OP.min)
+            if 0 < k < 7:
+                candidates(k)
+                cp(B("PQ", n, n + 8), B("OF", n, n + 8))
+            elif k == 7:
+                cp(B("PQ", n + 6, n + 8), B("OF", n + 6, n + 8))
+                cp(B("PQ", n, n + 2), B("OF", n, n + 2))
+                spare()
+            tt(B("GA"), B("SCP", o + E, o + 2 * E, ix=B("OF", n, n + 2)), B("GB"), OP.is_le)
+            if 0 < k < 7:
+                candidates_own(k)
+            if 0 < k < 6:
+                diff_ends(k)
+            if k > 3:
+                right_place(k)
+            spare()
+            scan(B("CS", c, c + 32), B("RM", 0, 32), B("GA"), OP.mult, OP.add)
+            if 0 < k < 7:
+                diff_candidates(k)
+            if k > 3:
+                place_diff(k)
+            if k < 7:
+                for x in range(4 if k < 6 else 0):
+                    ts(col("OF", n + 8 + (4 + x if x < 2 else x)), col("CS", c + 15 + 16 * (x % 2)), col("D2", 4 * k + x), OP.mult, col("PQ", n + 4 + x), OP.add)
+                spare()
+                for x in (2, 3, 0, 1):
+                    ts(col("OF", n + 8 + (4 + x if x > 1 else x)), col("CS", c + 15 + 16 * (x % 2)), col("D1", 4 * k + x), OP.mult,
+                       col("SCN", 128 * k + 79 + 16 * x), OP.add)
+                if k > 3:
+                    places(k)
+                elif k == 3:
+                    lists_out(0, 4, "exa")
+            else:
+                while soon:
+                    spare()
+                places(k)
+        while todo:
+            todo.pop(0)()
+
+        def flux(f, b):
+            f(B("M", b, 1024, 4), B("VP", E * b, E * b + E, ix=B("OFN")))
+
+        act(B("UNW"), B("IOTA", 0, E, ix=B("OFN")))
+        for b in range(2):
+            flux(cp, b)
+            flux(act, b + 2)
+        def equal(x):
+            tt(B("EE", 256 * x, 256 * x + 256), B("NI", ix=B("REP", 16 * x, 16 * x + 16)), B("UNW"), OP.is_equal)
+
+        cp(B("NI"), B("OFN"))
+        ts(B("T1"), B("NI"), 0x1F0, OP.bitwise_and)
+        equal(0)
+        quant("QM", "SM", 0, C, "M")
+        equal(1)
+        tt(B("CEA"), B("NI"), B("T1"), OP.add)
+        for x in range(2):
+            scan(B("DS", 256 * x, 256 * x + 256), B("EE", 256 * x, 256 * x + 256), B("CDG", 256 * x, 256 * x + 256), OP.max, OP.mult)
+        for x in range(2):
+            ts(B("FLB", x, 16, 2), B("DS", 256 * x + 31, 256 * x + 256, 32), B("PF", 6, 7) if x else B("PF", 2, 3), OP.mult)
+        tt(B("MXB"), B("CEA"), B("FLB"), OP.max)
+        ts(B("OFS"), B("MXB"), B("PF", 3, 4), OP.add)
+        cell = ("CELL%d" % (2 * t), "CELL%d" % (2 * t + 1))
+
+        def scatter(w):
+            cp(B(cell[w % 2], ix=B("OFS", 2 * w, 2 * w + 2)), B("POS", 32 * w, 32 * w + 32))
+
+        for w in range(PRE):
+            scatter(w)
+        for b in range(4):
+            act(B("TT", b, 1024, 4), mm("WQ", "WS", 128 * b, "QM", "SM", 0, C), scale=0.03125)
+        quant("QT", "SQ", 0, C, "TT")
+        for b in range(4):
+            act(B("DW", PW * b + 1, PW * b + 257), mm("QE", "SE", 128 * b, "QT", "SQ", 0, C), scale=-1.0)
+        for w in range(PRE, 8):
+            scatter(w)
+        for x in range(2):
+            run("v", v.transpose, B("CT%d" % x), B(cell[x], 0, 768))
+        for x in range(2):
+            tt(B("CB" if x else "CA"), B("CT%d" % x, 0, 768, 32), B("CT%d" % x, 16, 768, 32), OP.max)
+        tt(B("CM"), B("CA"), B("CB"), OP.max)
+        cp(B("OFC"), B("CM"))
+
+        def taken(b, w0, w1):
+            return B("DW", PW * b, PW * b + 257, ix=B("OFC", w0, w1))
+
+        for b in (0, 2, 1, 3):
+            if b < 2:
+                ts(B("UB", b, 512, 4), taken(b, 16, 24), -1.0, OP.mult)
+            else:
+                act(B("UB", b, 512, 4), taken(b, 16, 24), scale=-1.0)
+        quant("QB", "SB", 0, 128, "UB")
+        exchange(nxt, prv, ((B("LB", bit=dt.uint8), B("QB", bit=dt.uint8)), (B("LS"), B("SB"))), "bar", "sbar")
+        for b in range(4):
+            tt(B("X", 512 + b, 1024, 4), taken(b, 8, 16), B("VP", E * b + H, E * b + C), OP.add)
+        quant("QX", "SX", H, C, "X")
+        for b in range(4):
+            tt(B("FU", H * b, H * b + H), taken(b, 0, 8), B("VP", E * b, E * b + H), OP.add)
+
+        def result(a, b):
+            act(B("YO", a, b), mm("QV", "SV", 0, "QX", "SX", a, b))
+            sem = "outs" if a else "oute"
+            dma("y", sem, T.oc[:, 4 * a:4 * b], B("QX", a, b, bit=dt.uint8))
+            for k in range(4):
+                dma("s" if a == 0 and k % 2 else "y", sem, T.osc[4 * k:4 * k + 4, a:b], B("SX", a, b, p=(32 * k, 32 * k + 4)))
+            dma("s", sem, T.y[:, a:b], B("YO", a, b))
+
+        if last:
+            act(B("ONR"), B("UNW", ix=B("REV")))
+            dma("y", "outs", T.on[:], (T.ONR[0:128:16, :], B("ONR")[1]))
+            result(H, C)
+        else:
+            for k in range(EARLY):
+                score(k, H, C)
+        for b in range(4):
+            tt(B("X", b, 512, 4), B("FU", H * b, H * b + H), mm("QE", "SE", 128 * b, "LB", "LS", 0, H), OP.subtract)
+        quant("QX", "SX", 0, H, "X")
+        if last:
+            result(0, H)
+        else:
+            send_border()
+            for k in range(8):
+                score(k, 0, H if k < EARLY else C)
+    for sem in SEMAPHORES:
+        wait("g", sem, count[sem])

@@ -3,18 +3,17 @@ from concourse.mybir import dt, AluOpType, ActivationFunctionType
 OP = AluOpType
 AF = ActivationFunctionType
 N, R, C, H, E = 8, 3, 256, 128, 384
-CW = 816
+CW = 1024
 PW = 272
-EARLY = 4
-PRE = 2
-LISTS = ("float8_e4m3fn_x4 QX 384 QU 128 UQ 1024 QV 128 WQ 512 QE 512 QM 256 QT 256 QB 128 LB 128",
-         "uint8 SX 384 SU 128 US 1024 SV 128 WS 512 SE 512 SM 256 SQ 256 SB 128 LS 128",
-         "bfloat16 X 1024 UIN 512 VIN 512 ONES 512 EB 2048 VP 1536 M 1024 TT 1024 DW 1088 CELL0 816 CELL1 816 "
-         "CELL2 816 CELL3 816 CELL4 816 CELL5 816 POS 256 CT0 768 CT1 768 UB 512",
-         "float32 IOTA 768 TAB 6144 SCP 3456 PQ 64 SCN 1024 CS 256 GT 128 GB 32 GA 32 D1 32 D2 32 BU 16 AB 16 FA 16 NB 16 "
-         "UNW 256 CEA 16 EE 512 DS 512 FLB 16 MXB 16 CM 24 CA 24 CB 24 FU 512 MASK 128 MINM 32 RM 128 CDG 512 PF 8 YO 256 ONR 256",
-         "int32 LST 384 NI 16 T1 16 MD 128 MDA 128 ME 512 MF 512 MI 128 MJ 128 PI 8 UOI 64 RI 32",
-         "uint16 LSU 384 OF 64 NU 16 OFN 16 OFS 16 OFC 24 UOF 64 REP 32 REV 16")
+SEG = (0, 64, 112, 144, 160)
+LISTS = ("float8_e4m3fn_x4 QX 384 QU 128 UQ 128 QV 128 WQ 512 QE 512 QM 256 QT 256 QB 128 LB 128",
+         "uint8 SX 384 SU 128 US 128 SV 128 WS 512 SE 512 SM 256 SQ 256 SB 128 LS 128",
+         "bfloat16 X 1024 UIN 512 VIN 512 ONES 520 EB 520 VP 1536 M 1024 TT 1024 DW 1088 CELL0 1024 CELL1 1024 "
+         "CELL2 1024 POS 256 CT 768 UB 512 EE 640 DS 640 CDG 640",
+         "float32 IOTA 384 IOL 384 IOH 384 W2 768 NAT 768 TAB 768 SCP 384 GB 64 GA 64 GG 192 TG 768 TF 64 DD 128 "
+         "UNW 256 NF 16 CEA 16 CEB 16 FU 512 PF 32 YO 256 ONR 256",
+         "int32 LN 96 NI 16 T1 16 PI 8",
+         "uint16 LU 96 OF 128 OFI 4 CVC 4 NU 16 OFN 16 OFS 16 OFC 32 UOF 8 REV 16")
 WIDTH = {}
 SCRATCH = {}
 for _line in LISTS:
@@ -25,8 +24,8 @@ for _line in LISTS:
 for _i in range(8):
     WIDTH["ps%d" % _i] = 512
     SCRATCH["ps%d" % _i] = ("psum", [128, 512], "float32")
-SEMAPHORES = ["v", "s", "pe", "gp", "lx0", "lx1", "lu", "lv", "lwc", "lws", "la", "lb", "lr", "exa", "ex4", "ex5", "ex6",
-              "ex7", "outs", "oute", "brd", "bar", "sbrd", "sbar"]
+SEMAPHORES = ["v", "s", "pe", "gp", "lx0", "lx1", "lu", "lv", "lwc", "lws", "la", "lb", "tl", "tr", "outs", "oute",
+              "brd", "bar", "sbrd", "sbar"] + ["ex%d" % _i for _i in range(8)]
 
 
 def rank_program(g, core, T, topo):
@@ -77,8 +76,8 @@ def rank_program(g, core, T, topo):
             for r in regs:
                 log.setdefault(r[0], []).append((kind,) + r[1:] + (sem, count[sem], far))
 
-    def run(q, call, *args, outs=1, **kw):
-        reads, writes, real = [], [], []
+    def run(q, call, *args, outs=1, more=(), **kw):
+        reads, writes, real = list(more), [], []
         for i, x in enumerate(args):
             if isinstance(x, tuple):
                 (writes if i < outs else reads).extend(x[1])
@@ -123,19 +122,32 @@ def rank_program(g, core, T, topo):
         run("v", v.tensor_copy, out, in_)
 
     def act(out, in_, func=AF.Copy, **kw):
-        run("s", s.activation, out, in_, func, **kw)
+        if isinstance(kw.get("scale"), tuple):
+            run("s", s.activation, out, in_, func, more=kw["scale"][1], scale=kw["scale"][0])
+        else:
+            run("s", s.activation, out, in_, func, **kw)
+
+    def scaled(q, out, in_, c):
+        if q == "v":
+            ts(out, in_, c, OP.mult)
+        else:
+            act(out, in_, scale=c)
 
     def scan(out, d0, d1, op0, op1):
         run("v", v.tensor_tensor_scan, out, d0, d1, 0.0, op0, op1)
 
+    def turn(out, in_):
+        run("v", v.transpose, out, in_)
+
     def fill(x, c):
         run("v", v.memset, x, c)
 
-    def iota(out, step, n, base, cm):
-        run("g", g.iota, out, [[step, n]], base, cm, allow_small_or_imprecise_dtypes=True)
+    def iota(out, pattern, base, cm):
+        run("g", g.iota, out, pattern, base, cm, allow_small_or_imprecise_dtypes=True)
 
-    def quant(q, sc, a, b, tile):
-        run("v", v.quantize_mx, B(q, a, b), B(sc, a, b), B(tile, 4 * a, 4 * b), outs=2)
+    def quant(q, sc, a, b, tile, o=None):
+        o = 4 * a if o is None else o
+        run("v", v.quantize_mx, B(q, a, b), B(sc, a, b), B(tile, o, o + 4 * (b - a)), outs=2)
 
     bank = [0]
 
@@ -145,269 +157,285 @@ def rank_program(g, core, T, topo):
         run("pe", g.tensor.matmul_mx, B(p, 0, b - a), B(lq, la, la + 128), B(ls, la, la + 128), B(rq, a, b), B(rs, a, b), True, True)
         return B(p, 0, b - a)
 
-    def score(k, a, b):
-        o = E * (k + 1)
-        act(B("SCP", o + a, o + b), mm("UQ", "US", 128 * k, "QX", "SX", a, b), AF.Abs)
+    def score(a, b):
+        act(B("SCP", a, b), mm("UQ", "US", 0, "QX", "SX", a, b), AF.Abs)
+
+    def number(k, a, b):
+        act(B("VP", E * k + a, E * k + b), mm("QE", "SE", 128 * k, "QX", "SX", a, b))
 
     def send_border():
         exchange(prv, nxt, ((B("QX", C, E, bit=dt.uint8), B("QX", 0, H, bit=dt.uint8)), (B("SX", C, E), B("SX", 0, H))), "brd", "sbrd")
 
-    soon, todo = [], []
+    todo = []
 
-    def spare():
-        if soon:
-            soon.pop(0)()
+    def later(f, *a):
+        todo.append(lambda: f(*a))
 
-    def later(f, *a, to=todo):
-        to.append(lambda: f(*a))
-
-    dma("y", "lx0", B("X", 0, 512), T.x[:, 0:512])
-    dma("s", "lu", B("UIN"), T.u[:])
-    for k in range(8):
-        dma("y", "la", B("LST", 48 * k, 48 * k + 24, p=(0, 16)), T.lf[16 * k:16 * k + 16, :])
-        dma("s", "lb", B("LST", 48 * k + 24, 48 * k + 48, p=(0, 16)), T.rt[16 * k:16 * k + 16, :])
-    dma("y", "lx1", B("X", 512, 1024), T.x[:, 512:1024])
-    for h in range(1, 8):
-        dma("y", "lr", B("LST", p=(16 * h, 16 * h + 16)), B("LST", p=(0, 16)))
-    iota(B("IOTA", 0, E), 1, E, 0, 0)
-    iota(B("PI", 0, 1), 1, 1, 0, 1)
-    iota(B("IOTA", E, 2 * E), 1, E, E, 0)
-    fill(B("ONES"), 1.0)
-    cp(B("MI"), B("IOTA", 0, 128))
-    ts(B("UOI"), B("MI", 0, 64), 0x38, OP.bitwise_and)
-    ts(B("UOF"), B("UOI"), 2, OP.mult)
-    cp(B("PF", 0, 1), B("PI", 0, 1))
-    quant("QX", "SX", 0, H, "X")
-    send_border()
-    iota(B("SCP", 0, E), 1, E, 0, 0)
-    for b in range(4):
-        run("g", g.affine_select, B("EB", 512 * b, 512 * b + 512), B("ONES"), [[-8, 128], [-1, 4]], OP.is_equal, 0.0, b, 8)
-    iota(B("POS"), 1, 256, 1, 0)
-    for x in range(2 * R):
-        iota(B("CELL%d" % x), 0, CW, 0, 0)
-    dma("s", "lwc", B("WQ", bit=dt.uint8), T.wc[:])
-    dma("s", "lws", B("WS"), T.ws[:])
-    dma("y", "lv", B("VIN"), T.v[:])
-    quant("QU", "SU", 0, 128, "UIN")
-    cp(B("UQ", bit=dt.uint32), B("QU", bit=dt.uint32, ix=B("UOF")))
-    act(B("US"), B("SU", ix=B("UOF")))
-    quant("QX", "SX", H, C, "X")
-    for k in range(8):
-        score(k, 0, C)
-    ts(B("MD"), B("IOTA", 0, 128), B("PF", 0, 1), OP.subtract, 256.0, OP.add)
-    ts(B("PI", 1, 2), B("PI", 0, 1), 7, OP.bitwise_and)
-    ts(B("PI", 2, 3), B("PI", 0, 1), 3, OP.arith_shift_right)
-    ts(B("MDA"), B("MD"), 15, OP.bitwise_and)
-    ts(B("PF", 5, 6), B("PI", 1, 2), 32, OP.mult)
-    ts(B("MJ"), B("MI"), 15, OP.bitwise_and)
-    ts(B("MASK"), B("MDA"), 0, OP.is_equal)
-    tt(B("PF", 1, 2), B("PF", 5, 6), B("PI", 2, 3), OP.add)
-    ts(B("RM"), B("MJ"), 0, OP.not_equal)
-    ts(B("MINM"), B("MASK", 0, 32), 1e29, OP.mult, -1.0, OP.add)
-    for x in range(4):
-        ts(B("OF", 2 + x, 3 + x), B("PF", 1, 2), -1.0, OP.mult, float(255 - 16 * (x % 2) + E * (1 - x // 2)), OP.add)
-    cp(B("LSU"), B("LST"))
-
-    def table(q, k):
-        for x in range(2):
-            o, l = 768 * k + E * x, 48 * k + 24 * x
-            (cp if q == "v" else act)(B("TAB", o, o + E), B("IOTA", E * x, E * x + E, ix=B("LSU", l, l + 24)))
+    def spare(n=1):
+        for _ in range(n):
+            if todo:
+                todo.pop(0)()
 
     def col(buf, x):
         return B(buf, x, x + 1)
 
-    def candidates(k):
-        tt(B("GT"), B("TAB", 768 * k + 768, 768 * k + 1536, ix=B("OF", 8 * k, 8 * k + 8)), B("MASK"), OP.mult)
+    def pi(x):
+        return col("PI", x)
 
-    def candidates_own(k):
-        scan(B("SCN", 128 * k, 128 * k + 128), B("RM"), B("GT"), OP.mult, OP.add)
+    def pf(x):
+        return col("PF", x)
 
-    def diff_ends(k):
-        tt(B("D2", 4 * k, 4 * k + 4), B("PQ", 8 * k, 8 * k + 4), B("PQ", 8 * k + 4, 8 * k + 8), OP.subtract)
+    dma("y", "lx0", B("X", 0, 512), T.x[:, 0:512])
+    for q, sem, x, src in (("s", "la", 0, T.lf), ("y", "lb", 1, T.rt)):
+        dma(q, sem, B("LN", 48 * x, 48 * x + 24), src[:])
+        dma(q, sem, B("LN", 48 * x + 24, 48 * x + 48, p=(0, 112)), src[16:128, :])
+        dma(q, sem, B("LN", 48 * x + 24, 48 * x + 48, p=(112, 128)), src[0:16, :])
+    dma("s", "lu", B("UIN"), T.u[:])
+    dma("y", "lx1", B("X", 512, 1024), T.x[:, 512:1024])
+    dma("y", "lwc", B("WQ", bit=dt.uint8), T.wc[:])
+    dma("y", "lws", B("WS"), T.ws[:])
+    dma("y", "lv", B("VIN"), T.v[:])
+    iota(pi(0), [[1, 1]], 0, 1)
+    iota(B("IOTA"), [[1, E]], 0, 0)
+    fill(B("ONES"), 1.0)
+    run("g", g.affine_select, B("EB"), B("ONES"), [[-1, 520]], OP.is_equal, 0.0, 3, 4)
+    for x, (c, op) in enumerate(((7, OP.bitwise_and), (3, OP.arith_shift_right), (8, OP.bitwise_and), (16, OP.bitwise_and), (15, OP.bitwise_and))):
+        ts(pi(x + 1), pi(0), c, op)
+    ts(pf(0), pi(1), 16.0, OP.mult)
+    ts(pf(1), pi(3), 0.0, OP.is_equal)
+    ts(pf(2), pi(3), 0.0, OP.not_equal)
+    ts(pf(3), pi(1), -32.0, OP.mult, 255.0, OP.add)
+    ts(pf(4), pi(4), -0.875, OP.mult)
+    cp(pf(8), pi(5))
+    cp(pf(9), pi(4))
+    ts(B("UOF"), B("ONES", 0, 8), pf(0), OP.mult)
+    tt(pf(5), pf(3), pi(2), OP.subtract)
+    ts(B("IOL"), B("IOTA"), pf(2), OP.mult)
+    act(B("IOH"), B("IOTA"), scale=pf(1))
+    tt(pf(6), pf(5), pf(4), OP.add)
+    ts(pf(7), pf(5), float(E), OP.add)
+    act(B("TAB", 0, E), B("IOTA"))
+    act(B("TAB", E, 2 * E), B("IOTA"), AF.Identity, bias=float(E))
+    cp(B("LU", 0, 48), B("LN", 0, 48))
+    cp(B("LU", 48, 96), B("LN", 48, 96))
+    quant("QX", "SX", 0, H, "X")
+    send_border()
+    iota(B("POS"), [[1, 256]], 1, 0)
+    for x in range(R):
+        iota(B("CELL%d" % x), [[0, CW]], 0, 0)
 
-    def diff_candidates(k):
-        tt(B("D1", 4 * k, 4 * k + 4), B("SCN", 128 * k + 15, 128 * k + 64, 16), B("SCN", 128 * k + 79, 128 * k + 128, 16), OP.subtract)
+    def shifted(x):
+        tt(B("W2", E * x, E * x + E), B("IOL", ix=B("LU", 48 * x + 24, 48 * x + 48)), B("IOH"), OP.add)
 
-    table("v", 0)
-    tt(B("GT", 0, 64), B("TAB", 0, 768, ix=B("OF", 2, 6)), B("MASK", 0, 64), OP.mult)
-    scan(B("SCN", 0, 64), B("RM", 0, 64), B("GT", 0, 64), OP.mult, OP.add)
-    cp(B("OF", 6, 8), B("SCN", 15, 32, 16))
-    cp(B("OF", 0, 2), B("SCN", 47, 64, 16))
-    table("v", 1)
-    cp(B("PQ", 0, 8), B("OF", 0, 8))
-    candidates(0)
-    diff_ends(0)
-    candidates_own(0)
-    diff_candidates(0)
-    later(ts, B("PI", 3, 4), B("PI", 0, 1), 15, OP.bitwise_and)
-    later(ts, B("PI", 4, 5), B("PI", 0, 1), 16, OP.bitwise_and)
-    for x in range(2):
-        later(ts, B("RI", 16 * x, 16 * x + 16), B("MI", 0, 16), 14, OP.bitwise_and)
-    later(cp, B("PF", 4, 5), B("PI", 3, 4))
-    later(cp, B("PF", 3, 4), B("PI", 4, 5))
-    later(ts, B("PF", 2, 3), B("PI", 3, 4), 768, OP.add)
-    later(ts, B("PF", 6, 7), B("PI", 3, 4), 784, OP.add)
-    for x in range(2):
-        later(ts, B("ME", 256 * x, 256 * x + 256), B("IOTA", 0, 256), B("PF", 4, 5), OP.subtract, 256.0 - 16 * x, OP.add)
-        later(ts, B("REP", 16 * x, 16 * x + 16), B("RI", 16 * x, 16 * x + 16), x, OP.add)
-    later(ts, B("PF", 7, 8), B("PF", 4, 5), -1.0, OP.mult, 255.0, OP.add)
-    later(ts, B("MF"), B("ME"), 31, OP.bitwise_and)
-    later(quant, "QV", "SV", 0, 128, "VIN")
+    def tables(f, x):
+        f(B("NAT", E * x, E * x + E), B("W2", E * x, E * x + E, ix=B("LU", 48 * x, 48 * x + 24)))
+        for h in range(8):
+            dma("y", "tr" if x else "tl", B("TAB", E * x, E * x + E, p=(16 * h, 16 * h + 15)),
+                (T.NAT[h:120:8, E * x:E * x + E], B("NAT", E * x, E * x + E)[1]))
+
+    shifted(0)
+    tables(act, 0)
+    shifted(1)
+    quant("QU", "SU", 0, 128, "UIN")
+    ts(B("OF", 4, 6), B("IOTA", 0, 2), -16.0, OP.mult, pf(5), OP.add)
+    ts(B("OF", 6, 8), B("IOTA", 0, 2), -16.0, OP.mult, pf(7), OP.add)
+    ts(B("OFI", 0, 2), B("IOTA", 0, 2), -2.0, OP.mult, pf(6), OP.add)
+    tables(cp, 1)
+    ts(B("OFI", 2, 4), B("OFI", 0, 2), float(E), OP.add)
+    cp(B("UQ", bit=dt.uint32), B("QU", bit=dt.uint32, ix=B("UOF")))
+    act(B("US"), B("SU", ix=B("UOF")))
+    quant("QX", "SX", H, C, "X")
     for b in range(4):
-        later(fill, B("DW", PW * b, PW * b + 1), 0.0)
-    later(ts, B("CDG"), B("MF"), 0, OP.not_equal)
-    later(ts, B("REV"), B("IOTA", 0, 16), -16.0, OP.mult, B("PF", 7, 8), OP.add)
+        quant("QE", "SE", 128 * b, 128 * b + 128, "EB", 3 - b)
+    score(0, C)
+    for b in range(4):
+        number(b, 0, C)
 
-    def list_out(k, sem):
-        dma("y", sem, B("OFN", p=(16 * k, 16 * k + 16)), B("NU", 2 * k, 2 * k + 2))
+    def pair(k, c):
+        return B("TG", 96 * k + c, 96 * k + c + 17, 16)
 
-    def lists_out(k0, k1, sem):
-        def part(buf, j):
-            return B(buf, 2 * k0 + j, 2 * k1, 2)
+    def one(k, e, c):
+        return col("TG", 96 * k + 16 * e + c)
 
-        def end():
-            cp(B("NU", 2 * k0, 2 * k1), B("NB", 2 * k0, 2 * k1))
-            for k in range(k0, k1):
-                list_out(k, sem)
+    def width(k):
+        return 96 if k % 2 else 64
 
-        for j in range(2):
-            later(ts, part("BU", j), B("PQ", 8 * k0 + 6 + j, 8 * k1, 8), -float(E), OP.add, to=soon)
-        for j in range(2):
-            later(tt, part("AB", j), B("PQ", 8 * k0 + j, 8 * k1, 8), part("BU", j), OP.subtract, to=soon)
-        for j in range(2):
-            later(tt, part("FA", j), B("CS", 32 * k0 + 15 + 16 * j, 32 * k1, 32), part("AB", j), OP.mult, to=soon)
-        for j in range(2):
-            later(tt, part("NB", j), part("FA", j), part("BU", j), OP.add, to=soon)
-        later(end, to=soon)
+    def look(f, k):
+        f(B("GG", 96 * (k % 2), 96 * (k % 2) + width(k)), B("TAB", ix=B("OF", 16 * k + 4, 16 * k + 4 + width(k) // 16)))
 
-    def right_place(k):
-        ts(B("BU", 2 * k, 2 * k + 2), B("PQ", 8 * k + 6, 8 * k + 8), -float(E), OP.add)
+    def look_turn(k):
+        turn(B("TG", 96 * k, 96 * k + width(k)), B("GG", 96 * (k % 2), 96 * (k % 2) + width(k)))
 
-    def place_diff(k):
-        tt(B("AB", 2 * k, 2 * k + 2), B("PQ", 8 * k, 8 * k + 2), B("BU", 2 * k, 2 * k + 2), OP.subtract)
+    def diffs(k):
+        d = 16 * k
+        if k < 7:
+            tt(B("DD", d + 6, d + 8), pair(k, 34 + 2 * k), pair(k, 33 + 2 * k), OP.subtract)
+            tt(B("DD", d + 2, d + 4), pair(k, 2 * k + 1), pair(k, 2 * k + 2), OP.subtract)
+            tt(B("DD", d, d + 2), pair(k, 2 * k), pair(k, 15), OP.subtract)
+            for e in range(2):
+                ts(col("DD", d + 4 + e), one(k, e, 47), one(k, e, 32 + 2 * k), OP.subtract, -float(E), OP.add)
+            ts(B("DD", d + 10, d + 12), pair(k, 32 + 2 * k), float(E), OP.add)
+        tt(B("DD", d + 8, d + 10), pair(k, 2 * k), pair(k, 32 + 2 * k), OP.subtract)
 
-    def places(k):
-        for j in range(2):
-            ts(col("NU", 2 * k + j), col("CS", 32 * k + 15 + 16 * j), col("AB", 2 * k + j), OP.mult, col("BU", 2 * k + j), OP.add)
-        list_out(k, "ex%d" % k)
+    def list_out(k):
+        dma("y", "ex%d" % k, B("OFN", p=(16 * k, 16 * k + 16)), B("NU", 2 * k, 2 * k + 2))
+
+    cp(B("GB"), B("TAB", ix=B("OFI")))
+    look(cp, 0)
+    turn(B("TF"), B("GB"))
+    look_turn(0)
+    cp(B("OF", 0, 2), B("TF", 32, 64, 16))
+    cp(B("OF", 2, 4), B("TF", 0, 32, 16))
+    diffs(0)
+    later(ts, col("CVC", 0), pi(5), 32.0, OP.mult, pf(9), OP.add)
+    later(ts, col("CVC", 2), pi(1), 32.0, OP.mult, pf(9), OP.add)
+    later(ts, pf(10), pf(8), -1.0, OP.mult, 255.0, OP.add)
+    for i in range(4):
+        later(ts, pf(12 + i), pf(8), 4.0, OP.mult, 768.0 + 64 * i, OP.add)
+        later(ts, B("CDG", SEG[i], SEG[i + 1]), B("IOTA", 0, 64 - 16 * i), pf(8), OP.not_equal)
+    for b in range(4):
+        later(fill, col("DW", PW * b), 0.0)
+    for i in range(4):
+        later(ts, col("CDG", SEG[i + 1] - 1), col("CDG", SEG[i + 1] - 1), pf(12 + i), OP.mult)
+    later(ts, B("REV"), B("IOTA", 0, 16), -16.0, OP.mult, pf(10), OP.add)
+    later(cp, B("CDG", 160, 320), B("CDG", 0, 160))
+    later(quant, "QV", "SV", 0, 128, "VIN")
+    later(cp, B("CDG", 320, 640), B("CDG", 0, 320))
 
     for t in range(R):
         last = t == R - 1
-
-        def numbers():
-            for b in range(4):
-                act(B("VP", E * b, E * b + E), mm("QE", "SE", 128 * b, "QX", "SX", 0, E))
-
-        if t == 0:
-            table("s", 2)
+        score(C, E)
         for k in range(8):
-            score(k, C, E)
-            if t == 0 and 1 <= k < 6:
-                table("s", k + 2)
-        if t:
-            numbers()
-        for k in range(8):
-            if t == 0 and k == 3:
-                quant("QE", "SE", 0, 512, "EB")
-                numbers()
-            o, c, n = E * k, 32 * k, 8 * k
-            tt(B("GB"), B("SCP", o, o + 2 * E, ix=B("OF", n + 6, n + 8)), B("MINM"), OP.min)
-            if 0 < k < 7:
-                candidates(k)
-                cp(B("PQ", n, n + 8), B("OF", n, n + 8))
-            elif k == 7:
-                cp(B("PQ", n + 6, n + 8), B("OF", n + 6, n + 8))
-                cp(B("PQ", n, n + 2), B("OF", n, n + 2))
-                spare()
-            tt(B("GA"), B("SCP", o + E, o + 2 * E, ix=B("OF", n, n + 2)), B("GB"), OP.is_le)
-            if 0 < k < 7:
-                candidates_own(k)
-            if 0 < k < 6:
-                diff_ends(k)
-            if k > 3:
-                right_place(k)
+            n, c, d = 16 * k, 32 * (k % 2), 16 * k
+
+            def choose(out, x, e, y):
+                ts(out, col("DD", d + x + e), col("TF", c + 16 * e + k), OP.mult, y, OP.add)
+
+            cp(B("GB", c, c + 32), B("SCP", ix=B("OF", n, n + 2)))
+            if k:
+                look(act, k)
+            if k < 4:
+                number(k, C, E)
+            spare(2)
+            tt(B("GA", c, c + 32), B("SCP", ix=B("OF", n + 2, n + 4)), B("GB", c, c + 32), OP.is_le)
+            if k:
+                look_turn(k)
             spare()
-            scan(B("CS", c, c + 32), B("RM", 0, 32), B("GA"), OP.mult, OP.add)
-            if 0 < k < 7:
-                diff_candidates(k)
-            if k > 3:
-                place_diff(k)
+            turn(B("TF", c, c + 32), B("GA", c, c + 32))
+            if k:
+                diffs(k)
+            if k % 2:
+                cp(B("NU", 2 * k - 2, 2 * k), pair(k, 79))
+                list_out(k - 1)
+            spare()
+            for e in range(2):
+                if k < 7:
+                    choose(col("OF", n + 20 + e), 0, e, one(k, e, 15))
+                    choose(col("OF", n + 22 + e), 4, e, col("DD", d + 10 + e))
+                if k % 2 == 0:
+                    choose(col("OF", n + 24 + e), 8, e, one(k, e, 32 + 2 * k))
             if k < 7:
-                for x in range(4 if k < 6 else 0):
-                    ts(col("OF", n + 8 + (4 + x if x < 2 else x)), col("CS", c + 15 + 16 * (x % 2)), col("D2", 4 * k + x), OP.mult, col("PQ", n + 4 + x), OP.add)
-                spare()
-                for x in (2, 3, 0, 1):
-                    ts(col("OF", n + 8 + (4 + x if x > 1 else x)), col("CS", c + 15 + 16 * (x % 2)), col("D1", 4 * k + x), OP.mult,
-                       col("SCN", 128 * k + 79 + 16 * x), OP.add)
-                if k > 3:
-                    places(k)
-                elif k == 3:
-                    lists_out(0, 4, "exa")
-            else:
-                while soon:
-                    spare()
-                places(k)
-        while todo:
-            todo.pop(0)()
+                for e in range(2):
+                    choose(col("OF", n + 16 + e), 6, e, one(k, e, 33 + 2 * k))
+                for e in range(2):
+                    choose(col("OF", n + 18 + e), 2, e, one(k, e, 2 * k + 2))
+            if k % 2:
+                for e in range(2):
+                    choose(col("NU", 2 * k + e), 8, e, one(k, e, 32 + 2 * k))
+                list_out(k)
+        spare(99)
 
-        def flux(f, b):
-            f(B("M", b, 1024, 4), B("VP", E * b, E * b + E, ix=B("OFN")))
+        cell = "CELL%d" % t
 
-        act(B("UNW"), B("IOTA", 0, E, ix=B("OFN")))
-        for b in range(2):
-            flux(cp, b)
-            flux(act, b + 2)
-        def equal(x):
-            tt(B("EE", 256 * x, 256 * x + 256), B("NI", ix=B("REP", 16 * x, 16 * x + 16)), B("UNW"), OP.is_equal)
+        def unwrap(f, x):
+            f(B("UNW", 128 * x, 128 * x + 128), B("IOTA", ix=B("OFN", 8 * x, 8 * x + 8)))
+
+        def flux(f, b, x):
+            f(B("M", 512 * x + b, 512 * x + 512, 4), B("VP", E * b, E * b + E, ix=B("OFN", 8 * x, 8 * x + 8)))
+
+        def layer(x, qs):
+            quant("QM", "SM", H * x, H * x + H, "M")
+            for b in range(4):
+                scaled(qs[b], B("TT", 512 * x + b, 512 * x + 512, 4), mm("WQ", "WS", 128 * b, "QM", "SM", H * x, H * x + H), 0.03125)
+
+        def unpack(x, qs):
+            quant("QT", "SQ", H * x, H * x + H, "TT")
+            for b in range(4):
+                o = PW * b + 1 + H * x
+                scaled(qs[b], B("DW", o, o + H), mm("QE", "SE", 128 * b, "QT", "SQ", H * x, H * x + H), -1.0)
+
+        def equal(r):
+            for i in range(4):
+                ts(B("EE", 160 * r + SEG[i], 160 * r + SEG[i + 1]), B("UNW", 64 * r + 16 * i, 64 * r + 64), col("NF", 4 * r + i), OP.is_equal)
+
+        def later_equal(r):
+            scan(B("DS", 160 * r, 160 * r + 160), B("EE", 160 * r, 160 * r + 160), B("CDG", 160 * r, 160 * r + 160), OP.max, OP.mult)
+
+        def target(r):
+            for i in range(4):
+                ts(col("OFS", 4 * r + i), col("DS", 160 * r + SEG[i + 1] - 1), col("CEB", 4 * r + i), OP.max)
+
+        def scatter(r):
+            cp(B(cell, ix=B("OFS", 4 * r, 4 * r + 4)), B("POS", 64 * r, 64 * r + 64))
 
         cp(B("NI"), B("OFN"))
+        cp(B("NF"), B("OFN"))
+        unwrap(cp, 0)
+        for b in (2, 3):
+            flux(act, b, 0)
         ts(B("T1"), B("NI"), 0x1F0, OP.bitwise_and)
-        equal(0)
-        quant("QM", "SM", 0, C, "M")
-        equal(1)
+        flux(cp, 0, 0)
         tt(B("CEA"), B("NI"), B("T1"), OP.add)
-        for x in range(2):
-            scan(B("DS", 256 * x, 256 * x + 256), B("EE", 256 * x, 256 * x + 256), B("CDG", 256 * x, 256 * x + 256), OP.max, OP.mult)
-        for x in range(2):
-            ts(B("FLB", x, 16, 2), B("DS", 256 * x + 31, 256 * x + 256, 32), B("PF", 6, 7) if x else B("PF", 2, 3), OP.mult)
-        tt(B("MXB"), B("CEA"), B("FLB"), OP.max)
-        ts(B("OFS"), B("MXB"), B("PF", 3, 4), OP.add)
-        cell = ("CELL%d" % (2 * t), "CELL%d" % (2 * t + 1))
-
-        def scatter(w):
-            cp(B(cell[w % 2], ix=B("OFS", 2 * w, 2 * w + 2)), B("POS", 32 * w, 32 * w + 32))
-
-        for w in range(PRE):
-            scatter(w)
-        for b in range(4):
-            act(B("TT", b, 1024, 4), mm("WQ", "WS", 128 * b, "QM", "SM", 0, C), scale=0.03125)
-        quant("QT", "SQ", 0, C, "TT")
-        for b in range(4):
-            act(B("DW", PW * b + 1, PW * b + 257), mm("QE", "SE", 128 * b, "QT", "SQ", 0, C), scale=-1.0)
-        for w in range(PRE, 8):
-            scatter(w)
-        for x in range(2):
-            run("v", v.transpose, B("CT%d" % x), B(cell[x], 0, 768))
-        for x in range(2):
-            tt(B("CB" if x else "CA"), B("CT%d" % x, 0, 768, 32), B("CT%d" % x, 16, 768, 32), OP.max)
-        tt(B("CM"), B("CA"), B("CB"), OP.max)
-        cp(B("OFC"), B("CM"))
+        flux(cp, 1, 0)
+        unwrap(act, 1)
+        for b in (1, 2, 3):
+            flux(act, b, 1)
+        ts(B("CEB"), B("CEA"), pf(9), OP.add)
+        equal(0)
+        layer(0, "ssss")
+        later_equal(0)
+        flux(cp, 0, 1)
+        target(0)
+        equal(1)
+        scatter(0)
+        later_equal(1)
+        layer(1, "ssss")
+        target(1)
+        equal(2)
+        scatter(1)
+        later_equal(2)
+        unpack(0, "ssss")
+        target(2)
+        equal(3)
+        scatter(2)
+        later_equal(3)
+        unpack(1, "ssss")
+        target(3)
+        scatter(3)
+        turn(B("CT", 512, 768), B(cell, 512, 768))
+        turn(B("CT", 0, 512), B(cell, 0, 512))
+        cp(B("OFC", 16, 32), B("CT", 512, 768, ix=B("CVC", 2, 3)))
+        cp(B("OFC", 0, 16), B("CT", 0, 512, ix=B("CVC", 0, 1)))
 
         def taken(b, w0, w1):
             return B("DW", PW * b, PW * b + 257, ix=B("OFC", w0, w1))
 
         for b in (0, 2, 1, 3):
-            if b < 2:
-                ts(B("UB", b, 512, 4), taken(b, 16, 24), -1.0, OP.mult)
-            else:
-                act(B("UB", b, 512, 4), taken(b, 16, 24), scale=-1.0)
+            scaled("v" if b < 2 else "s", B("UB", b, 512, 4), taken(b, 16, 24), -1.0)
+
+        def low(b):
+            tt(B("FU", H * b, H * b + H), taken(b, 0, 8), B("VP", E * b, E * b + H), OP.add)
+
+        def high(b):
+            tt(B("X", 512 + b, 1024, 4), taken(b, 8, 16), B("VP", E * b + H, E * b + C), OP.add)
+
+        low(0)
         quant("QB", "SB", 0, 128, "UB")
         exchange(nxt, prv, ((B("LB", bit=dt.uint8), B("QB", bit=dt.uint8)), (B("LS"), B("SB"))), "bar", "sbar")
+        for b in range(1, 4):
+            low(b)
         for b in range(4):
-            tt(B("X", 512 + b, 1024, 4), taken(b, 8, 16), B("VP", E * b + H, E * b + C), OP.add)
-        quant("QX", "SX", H, C, "X")
-        for b in range(4):
-            tt(B("FU", H * b, H * b + H), taken(b, 0, 8), B("VP", E * b, E * b + H), OP.add)
+            high(b)
 
         def result(a, b):
             act(B("YO", a, b), mm("QV", "SV", 0, "QX", "SX", a, b))
@@ -420,18 +448,21 @@ def rank_program(g, core, T, topo):
         if last:
             act(B("ONR"), B("UNW", ix=B("REV")))
             dma("y", "outs", T.on[:], (T.ONR[0:128:16, :], B("ONR")[1]))
+            quant("QX", "SX", H, C, "X")
+        back = [mm("QE", "SE", 128 * b, "LB", "LS", 0, H) for b in range(4)]
+        if last:
             result(H, C)
-        else:
-            for k in range(EARLY):
-                score(k, H, C)
         for b in range(4):
-            tt(B("X", b, 512, 4), B("FU", H * b, H * b + H), mm("QE", "SE", 128 * b, "LB", "LS", 0, H), OP.subtract)
+            tt(B("X", b, 512, 4), B("FU", H * b, H * b + H), back[b], OP.subtract)
+        if not last:
+            quant("QX", "SX", H, C, "X")
         quant("QX", "SX", 0, H, "X")
         if last:
             result(0, H)
         else:
             send_border()
-            for k in range(8):
-                score(k, 0, H if k < EARLY else C)
+            score(0, C)
+            for b in range(4):
+                number(b, 0, C)
     for sem in SEMAPHORES:
         wait("g", sem, count[sem])

@@ -6,14 +6,18 @@ N, R, C, H, E = 8, 3, 256, 128, 384
 CW = 1024
 PW = 272
 SEG = (0, 64, 112, 144, 160)
+EARLY = "ha co ca eq0 eq1+cb la0 la1+ta0 ta1 sc0 no sc1 ly201 pi10 bo10"
+FLUX = ("ha ms23567 mv0 co mv1 ca eq0 qm0 ts0123 cb eq1 la0 mv4 ta0 la1 qm1 ts4567 sc0 ta1 qt0 ds0123 sc1 qt1 ly2 ly01 ds45 pi1 pi0 dv67 "
+        "bo1 bo0 uv0 us2 uv1 us3 lo0 qb on lo123 hi0123 bk qx1 qx0")
+LAST = FLUX.replace("bk qx1", "qx1 bk")
 LISTS = ("float8_e4m3fn_x4 QX 384 QU 128 UQ 128 QV 128 WQ 512 QE 512 QM 256 QT 256 QB 128 LB 128",
          "uint8 SX 384 SU 128 US 128 SV 128 WS 512 SE 512 SM 256 SQ 256 SB 128 LS 128",
          "bfloat16 X 1024 UIN 512 VIN 512 ONES 520 EB 520 VP 1536 M 1024 TT 1024 DW 1088 CELL0 1024 CELL1 1024 "
-         "CELL2 1024 POS 256 CT 768 UB 512 EE 640 DS 640 CDG 640",
-         "float32 IOTA 384 IOL 384 IOH 384 W2 768 NAT 768 TAB 768 SCP 384 GB 64 GA 64 GG 192 TG 768 TF 64 DD 128 "
-         "UNW 256 NF 16 CEA 16 CEB 16 FU 512 PF 32 YO 256 ONR 256",
+         "CELL2 1024 CELL3 1024 CELL4 1024 CELL5 1024 POS 128 CT 1536 UB 512 EE 640 DS 640 CDG 320",
+         "float32 IOTA 384 IOL 384 IOH 384 WA 768 WB 768 NAT 768 TAB 1536 SCP 384 GB 64 GA 64 GG 192 TG 768 TF 64 DD 16 "
+         "UNW 256 UNN 256 NF 16 CEA 16 CEB 16 CG 64 CM 32 FU 512 PF 32 YO 256 ONR 256",
          "int32 LN 96 NI 16 T1 16 PI 8",
-         "uint16 LU 96 OF 128 OFI 4 CVC 4 NU 16 OFN 16 OFS 16 OFC 32 UOF 8 REV 16")
+         "uint16 LU 96 OF 128 OFI 2 CVC 4 NU 16 OFN 16 OFD 16 OFS 16 OFC 24 UOF 8 REV 16")
 WIDTH = {}
 SCRATCH = {}
 for _line in LISTS:
@@ -24,7 +28,7 @@ for _line in LISTS:
 for _i in range(8):
     WIDTH["ps%d" % _i] = 512
     SCRATCH["ps%d" % _i] = ("psum", [128, 512], "float32")
-SEMAPHORES = ["v", "s", "pe", "gp", "lx0", "lx1", "lu", "lv", "lwc", "lws", "la", "lb", "tl", "tr", "outs", "oute",
+SEMAPHORES = ["v", "s", "pe", "gp", "lx0", "lx1", "lu", "lv", "lwc", "lws", "la", "lb", "t0", "t1", "outs", "oute",
               "brd", "bar", "sbrd", "sbar"] + ["ex%d" % _i for _i in range(8)]
 
 
@@ -198,98 +202,93 @@ def rank_program(g, core, T, topo):
     iota(pi(0), [[1, 1]], 0, 1)
     iota(B("IOTA"), [[1, E]], 0, 0)
     fill(B("ONES"), 1.0)
-    run("g", g.affine_select, B("EB"), B("ONES"), [[-1, 520]], OP.is_equal, 0.0, 3, 4)
-    for x, (c, op) in enumerate(((7, OP.bitwise_and), (3, OP.arith_shift_right), (8, OP.bitwise_and), (16, OP.bitwise_and), (15, OP.bitwise_and))):
+    for x, (c, op) in enumerate(((7, OP.bitwise_and), (3, OP.arith_shift_right), (8, OP.bitwise_and), (16, OP.bitwise_and),
+                                 (15, OP.bitwise_and), (4, OP.bitwise_and), (64, OP.bitwise_and))):
         ts(pi(x + 1), pi(0), c, op)
+    ts(pf(11), pi(6), -0.5, OP.mult, 1.0, OP.add)
     ts(pf(0), pi(1), 16.0, OP.mult)
-    ts(pf(1), pi(3), 0.0, OP.is_equal)
-    ts(pf(2), pi(3), 0.0, OP.not_equal)
     ts(pf(3), pi(1), -32.0, OP.mult, 255.0, OP.add)
     ts(pf(4), pi(4), -0.875, OP.mult)
+    ts(pf(7), pi(6), -0.25, OP.mult)
     cp(pf(8), pi(5))
     cp(pf(9), pi(4))
+    ts(pf(1), pi(3), 0.0, OP.is_equal, pf(11), OP.mult)
+    ts(pf(2), pi(3), 0.0, OP.not_equal, pf(11), OP.mult)
     ts(B("UOF"), B("ONES", 0, 8), pf(0), OP.mult)
     tt(pf(5), pf(3), pi(2), OP.subtract)
     ts(B("IOL"), B("IOTA"), pf(2), OP.mult)
     act(B("IOH"), B("IOTA"), scale=pf(1))
     tt(pf(6), pf(5), pf(4), OP.add)
-    ts(pf(7), pf(5), float(E), OP.add)
-    act(B("TAB", 0, E), B("IOTA"))
-    act(B("TAB", E, 2 * E), B("IOTA"), AF.Identity, bias=float(E))
     cp(B("LU", 0, 48), B("LN", 0, 48))
     cp(B("LU", 48, 96), B("LN", 48, 96))
     quant("QX", "SX", 0, H, "X")
     send_border()
-    iota(B("POS"), [[1, 256]], 1, 0)
-    for x in range(R):
-        iota(B("CELL%d" % x), [[0, CW]], 0, 0)
+    run("g", g.affine_select, B("EB"), B("ONES"), [[-1, 520]], OP.is_equal, 0.0, 3, 4)
+    for x in range(2 * R):
+        iota(B("CELL%d" % x, 0, 768), [[0, 768]], 0, 0)
 
     def shifted(x):
-        tt(B("W2", E * x, E * x + E), B("IOL", ix=B("LU", 48 * x + 24, 48 * x + 48)), B("IOH"), OP.add)
+        tt(B("WA", E * x, E * x + E), B("IOL", ix=B("LU", 48 * x + 24, 48 * x + 48)), B("IOH"), OP.add)
+        act(B("WB", E * x, E * x + E), B("WA", E * x, E * x + E), scale=pf(7))
 
-    def tables(f, x):
-        f(B("NAT", E * x, E * x + E), B("W2", E * x, E * x + E, ix=B("LU", 48 * x, 48 * x + 24)))
-        for h in range(8):
-            dma("y", "tr" if x else "tl", B("TAB", E * x, E * x + E, p=(16 * h, 16 * h + 15)),
-                (T.NAT[h:120:8, E * x:E * x + E], B("NAT", E * x, E * x + E)[1]))
+    def tables(x):
+        a, b = ("WA", "WB") if x else ("WB", "WA")
+        tt(B("NAT", E * x, E * x + E), B(a, E * x, E * x + E, ix=B("LU", 48 * x, 48 * x + 24)), B(b, E * x, E * x + E), OP.add)
 
     shifted(0)
-    tables(act, 0)
     shifted(1)
     quant("QU", "SU", 0, 128, "UIN")
-    ts(B("OF", 4, 6), B("IOTA", 0, 2), -16.0, OP.mult, pf(5), OP.add)
-    ts(B("OF", 6, 8), B("IOTA", 0, 2), -16.0, OP.mult, pf(7), OP.add)
-    ts(B("OFI", 0, 2), B("IOTA", 0, 2), -2.0, OP.mult, pf(6), OP.add)
-    tables(cp, 1)
-    ts(B("OFI", 2, 4), B("OFI", 0, 2), float(E), OP.add)
+    tables(0)
+    tables(1)
+    for x in range(2):
+        for h in range(8):
+            o = 64 * x + h % 4
+            dma("s" if x == 0 and h % 2 else "y", "t%d" % x, B("TAB", 2 * E * x, 2 * E * x + 2 * E, p=(16 * h, 16 * h + 16)),
+                (T.NAT[o:o + 61:4, :], B("NAT")[1]))
     cp(B("UQ", bit=dt.uint32), B("QU", bit=dt.uint32, ix=B("UOF")))
     act(B("US"), B("SU", ix=B("UOF")))
+    for x in range(2):
+        ts(B("OF", 4 + 2 * x, 6 + 2 * x), B("IOTA", 0, 2), -16.0, OP.mult, pf(5), OP.add)
+    ts(B("OFI"), B("IOTA", 0, 2), -2.0, OP.mult, pf(6), OP.add)
     quant("QX", "SX", H, C, "X")
     for b in range(4):
         quant("QE", "SE", 128 * b, 128 * b + 128, "EB", 3 - b)
     score(0, C)
-    for b in range(4):
-        number(b, 0, C)
 
-    def pair(k, c):
-        return B("TG", 96 * k + c, 96 * k + c + 17, 16)
-
-    def one(k, e, c):
-        return col("TG", 96 * k + 16 * e + c)
+    def one(k, e, x, i):
+        return col("TG", 96 * k + 32 * x + 16 * e + 4 * (k % 4) + i)
 
     def width(k):
         return 96 if k % 2 else 64
 
     def look(f, k):
-        f(B("GG", 96 * (k % 2), 96 * (k % 2) + width(k)), B("TAB", ix=B("OF", 16 * k + 4, 16 * k + 4 + width(k) // 16)))
+        o, c, n = 2 * E * (k // 4), 96 * (k % 2), 16 * k
+        f(B("GG", c, c + 32), B("TAB", o + E, o + 2 * E, ix=B("OF", n + 4, n + 6)))
+        f(B("GG", c + 32, c + width(k)), B("TAB", o, o + E, ix=B("OF", n + 6, n + 4 + width(k) // 16)))
 
     def look_turn(k):
         turn(B("TG", 96 * k, 96 * k + width(k)), B("GG", 96 * (k % 2), 96 * (k % 2) + width(k)))
 
-    def diffs(k):
-        d = 16 * k
-        if k < 7:
-            tt(B("DD", d + 6, d + 8), pair(k, 34 + 2 * k), pair(k, 33 + 2 * k), OP.subtract)
-            tt(B("DD", d + 2, d + 4), pair(k, 2 * k + 1), pair(k, 2 * k + 2), OP.subtract)
-            tt(B("DD", d, d + 2), pair(k, 2 * k), pair(k, 15), OP.subtract)
-            for e in range(2):
-                ts(col("DD", d + 4 + e), one(k, e, 47), one(k, e, 32 + 2 * k), OP.subtract, -float(E), OP.add)
-            ts(B("DD", d + 10, d + 12), pair(k, 32 + 2 * k), float(E), OP.add)
-        tt(B("DD", d + 8, d + 10), pair(k, 2 * k), pair(k, 32 + 2 * k), OP.subtract)
+    def a_less_b(k):
+        for e in range(2):
+            ts(col("DD", 2 * k + e), one(k, e, 1, 1), one(k, e, 1, 0), OP.add, one(k, e, 0, 0), OP.subtract)
 
     def list_out(k):
         dma("y", "ex%d" % k, B("OFN", p=(16 * k, 16 * k + 16)), B("NU", 2 * k, 2 * k + 2))
 
-    cp(B("GB"), B("TAB", ix=B("OFI")))
-    look(cp, 0)
+    for x in range(2):
+        cp(B("GB", 32 * x, 32 * x + 32), B("TAB", E * x, E * x + E, ix=B("OFI")))
+    look(act, 0)
     turn(B("TF"), B("GB"))
     look_turn(0)
     cp(B("OF", 0, 2), B("TF", 32, 64, 16))
-    cp(B("OF", 2, 4), B("TF", 0, 32, 16))
-    diffs(0)
+    for e in range(2):
+        ts(col("OF", 2 + e), col("TF", 16 * e), col("TF", 16 * e + 1), OP.add)
+    a_less_b(0)
     later(ts, col("CVC", 0), pi(5), 32.0, OP.mult, pf(9), OP.add)
     later(ts, col("CVC", 2), pi(1), 32.0, OP.mult, pf(9), OP.add)
     later(ts, pf(10), pf(8), -1.0, OP.mult, 255.0, OP.add)
+    later(ts, pf(16), pi(7), 2.0, OP.mult, 1.0, OP.add)
     for i in range(4):
         later(ts, pf(12 + i), pf(8), 4.0, OP.mult, 768.0 + 64 * i, OP.add)
         later(ts, B("CDG", SEG[i], SEG[i + 1]), B("IOTA", 0, 64 - 16 * i), pf(8), OP.not_equal)
@@ -297,131 +296,130 @@ def rank_program(g, core, T, topo):
         later(fill, col("DW", PW * b), 0.0)
     for i in range(4):
         later(ts, col("CDG", SEG[i + 1] - 1), col("CDG", SEG[i + 1] - 1), pf(12 + i), OP.mult)
-    later(ts, B("REV"), B("IOTA", 0, 16), -16.0, OP.mult, pf(10), OP.add)
+    later(ts, B("POS"), B("IOTA", 0, 128), pf(16), OP.add)
     later(cp, B("CDG", 160, 320), B("CDG", 0, 160))
+    later(ts, B("REV"), B("IOTA", 0, 16), -16.0, OP.mult, pf(10), OP.add)
     later(quant, "QV", "SV", 0, 128, "VIN")
-    later(cp, B("CDG", 320, 640), B("CDG", 0, 320))
+
+    def inverse(t, z, unwrap):
+        cell, o, p = "CELL%d" % (2 * t + z), 8 * z, (64 * z, 64 * z + 64)
+
+        def halves():
+            for x in range(2):
+                cp(B("OFD", o, o + 8, p=(64 * x, 64 * x + 64)), B("OFN", 8 * x, 8 * x + 8, p=p))
+
+        def copies():
+            unwrap(B("UNW", 128 * z, 128 * z + 128), B("IOTA", ix=B("OFD", o, o + 8)))
+            cp(B("NI", o, o + 8), B("OFD", o, o + 8))
+            cp(B("NF", o, o + 8), B("OFD", o, o + 8))
+            ts(B("CEA", o, o + 8), B("OFD", o, o + 8), pf(9), OP.add)
+
+        def equal(r):
+            for i in range(4):
+                a, u = 320 * z + 160 * r, 128 * z + 64 * r
+                ts(B("EE", a + SEG[i], a + SEG[i + 1]), B("UNW", u + 16 * i, u + 64), col("NF", o + 4 * r + i), OP.is_equal)
+
+        def later_equal(r):
+            a = 320 * z + 160 * r
+            scan(B("DS", a, a + 160), B("EE", a, a + 160), B("CDG", 160 * r, 160 * r + 160), OP.max, OP.mult)
+
+        def target(r):
+            for i in range(4):
+                c = o + 4 * r + i
+                ts(col("OFS", c), col("DS", 320 * z + 160 * r + SEG[i + 1] - 1), col("CEB", c), OP.max)
+
+        def scatter(r):
+            cp(B(cell, ix=B("OFS", o + 4 * r, o + 4 * r + 4)), B("POS", 64 * r, 64 * r + 64))
+
+        def lay(x):
+            turn(B("CT", 768 * z + 256 * x, 768 * z + 256 * x + 256), B(cell, 256 * x, 256 * x + 256))
+
+        def pick(x):
+            a = 768 * z + 512 * x
+            cp(B("CG", 32 * z + 16 * x, 32 * z + 16 * x + 16), B("CT", a, a + 512 - 256 * x, ix=B("CVC", 2 * x, 2 * x + 1)))
+
+        def both(x):
+            a, n = 32 * z + 16 * x, 16 - 8 * x
+            tt(B("CM", 16 * x, 16 * x + n, p=p), B("CG", a, a + n, p=(0, 64)), B("CG", a, a + n, p=(64, 128)), OP.max)
+            wait("v", "v", count["v"])
+            cp(B("OFC", 16 * x, 16 * x + n, p=p), B("CM", 16 * x, 16 * x + n, p=p))
+
+        return {"ha": lambda x: halves(), "co": lambda x: copies(), "eq": equal, "la": later_equal, "ta": target, "sc": scatter,
+                "ca": lambda x: ts(B("T1", o, o + 8), B("NI", o, o + 8), 0x1F0, OP.bitwise_and),
+                "cb": lambda x: tt(B("CEB", o, o + 8), B("CEA", o, o + 8), B("T1", o, o + 8), OP.add),
+                "ly": lay, "pi": pick, "bo": both, "no": lambda x: None}
+
+    def play(calls, word):
+        for name in word.split("+"):
+            for x in name[2:] or "0":
+                calls[name[:2]](int(x))
 
     for t in range(R):
         last = t == R - 1
         score(C, E)
         for k in range(8):
-            n, c, d = 16 * k, 32 * (k % 2), 16 * k
+            n, c = 16 * k, 32 * (k % 2)
+            if k == 5:
+                spare(99)
+                early = inverse(t, 0, act)
+                for word in EARLY.split():
+                    later(play, early, word)
 
-            def choose(out, x, e, y):
-                ts(out, col("DD", d + x + e), col("TF", c + 16 * e + k), OP.mult, y, OP.add)
+            def choose(out, d, e, y):
+                ts(out, d, col("TF", c + 16 * e + k), OP.mult, y, OP.add)
 
             cp(B("GB", c, c + 32), B("SCP", ix=B("OF", n, n + 2)))
             if k:
                 look(act, k)
             if k < 4:
-                number(k, C, E)
-            spare(2)
+                number(k, C if t else 0, E)
+            spare(2 if k < 5 else 1)
             tt(B("GA", c, c + 32), B("SCP", ix=B("OF", n + 2, n + 4)), B("GB", c, c + 32), OP.is_le)
             if k:
                 look_turn(k)
             spare()
             turn(B("TF", c, c + 32), B("GA", c, c + 32))
             if k:
-                diffs(k)
+                a_less_b(k)
             if k % 2:
-                cp(B("NU", 2 * k - 2, 2 * k), pair(k, 79))
+                cp(B("NU", 2 * k - 2, 2 * k), B("TG", 96 * k + 64, 96 * k + 96, 16))
                 list_out(k - 1)
             spare()
-            for e in range(2):
-                if k < 7:
-                    choose(col("OF", n + 20 + e), 0, e, one(k, e, 15))
-                    choose(col("OF", n + 22 + e), 4, e, col("DD", d + 10 + e))
-                if k % 2 == 0:
-                    choose(col("OF", n + 24 + e), 8, e, one(k, e, 32 + 2 * k))
             if k < 7:
-                for e in range(2):
-                    choose(col("OF", n + 16 + e), 6, e, one(k, e, 33 + 2 * k))
-                for e in range(2):
-                    choose(col("OF", n + 18 + e), 2, e, one(k, e, 2 * k + 2))
+                for x, i, o in ((0, 2, 16), (0, 0, 20), (1, 0, 22), (1, 2, 18)):
+                    for e in range(2):
+                        choose(col("OF", n + o + e), one(k, e, x, i + 1), e, one(k, e, x, i))
+            for e in range(2):
+                choose(col("NU", 2 * k + e) if k % 2 else col("OF", n + 24 + e), col("DD", 2 * k + e), e, one(k, e, 0, 0))
             if k % 2:
-                for e in range(2):
-                    choose(col("NU", 2 * k + e), 8, e, one(k, e, 32 + 2 * k))
                 list_out(k)
+            spare()
         spare(99)
-
-        cell = "CELL%d" % t
-
-        def unwrap(f, x):
-            f(B("UNW", 128 * x, 128 * x + 128), B("IOTA", ix=B("OFN", 8 * x, 8 * x + 8)))
 
         def flux(f, b, x):
             f(B("M", 512 * x + b, 512 * x + 512, 4), B("VP", E * b, E * b + E, ix=B("OFN", 8 * x, 8 * x + 8)))
 
-        def layer(x, qs):
+        made = {}
+
+        def layer(x):
             quant("QM", "SM", H * x, H * x + H, "M")
             for b in range(4):
-                scaled(qs[b], B("TT", 512 * x + b, 512 * x + 512, 4), mm("WQ", "WS", 128 * b, "QM", "SM", H * x, H * x + H), 0.03125)
+                made["t", 4 * x + b] = mm("WQ", "WS", 128 * b, "QM", "SM", H * x, H * x + H)
 
-        def unpack(x, qs):
+        def unpack(x):
             quant("QT", "SQ", H * x, H * x + H, "TT")
             for b in range(4):
-                o = PW * b + 1 + H * x
-                scaled(qs[b], B("DW", o, o + H), mm("QE", "SE", 128 * b, "QT", "SQ", H * x, H * x + H), -1.0)
+                made["d", 4 * x + b] = mm("QE", "SE", 128 * b, "QT", "SQ", H * x, H * x + H)
 
-        def equal(r):
-            for i in range(4):
-                ts(B("EE", 160 * r + SEG[i], 160 * r + SEG[i + 1]), B("UNW", 64 * r + 16 * i, 64 * r + 64), col("NF", 4 * r + i), OP.is_equal)
+        def layer_out(q, x):
+            scaled(q, B("TT", 512 * (x // 4) + x % 4, 512 * (x // 4) + 512, 4), made["t", x], 0.03125)
 
-        def later_equal(r):
-            scan(B("DS", 160 * r, 160 * r + 160), B("EE", 160 * r, 160 * r + 160), B("CDG", 160 * r, 160 * r + 160), OP.max, OP.mult)
-
-        def target(r):
-            for i in range(4):
-                ts(col("OFS", 4 * r + i), col("DS", 160 * r + SEG[i + 1] - 1), col("CEB", 4 * r + i), OP.max)
-
-        def scatter(r):
-            cp(B(cell, ix=B("OFS", 4 * r, 4 * r + 4)), B("POS", 64 * r, 64 * r + 64))
-
-        cp(B("NI"), B("OFN"))
-        cp(B("NF"), B("OFN"))
-        unwrap(cp, 0)
-        for b in (2, 3):
-            flux(act, b, 0)
-        ts(B("T1"), B("NI"), 0x1F0, OP.bitwise_and)
-        flux(cp, 0, 0)
-        tt(B("CEA"), B("NI"), B("T1"), OP.add)
-        flux(cp, 1, 0)
-        unwrap(act, 1)
-        for b in (1, 2, 3):
-            flux(act, b, 1)
-        ts(B("CEB"), B("CEA"), pf(9), OP.add)
-        equal(0)
-        layer(0, "ssss")
-        later_equal(0)
-        flux(cp, 0, 1)
-        target(0)
-        equal(1)
-        scatter(0)
-        later_equal(1)
-        layer(1, "ssss")
-        target(1)
-        equal(2)
-        scatter(1)
-        later_equal(2)
-        unpack(0, "ssss")
-        target(2)
-        equal(3)
-        scatter(2)
-        later_equal(3)
-        unpack(1, "ssss")
-        target(3)
-        scatter(3)
-        turn(B("CT", 512, 768), B(cell, 512, 768))
-        turn(B("CT", 0, 512), B(cell, 0, 512))
-        cp(B("OFC", 16, 32), B("CT", 512, 768, ix=B("CVC", 2, 3)))
-        cp(B("OFC", 0, 16), B("CT", 0, 512, ix=B("CVC", 0, 1)))
+        def unpack_out(q, x):
+            o = PW * (x % 4) + 1 + H * (x // 4)
+            scaled(q, B("DW", o, o + H), made["d", x], -1.0)
 
         def taken(b, w0, w1):
             return B("DW", PW * b, PW * b + 257, ix=B("OFC", w0, w1))
-
-        for b in (0, 2, 1, 3):
-            scaled("v" if b < 2 else "s", B("UB", b, 512, 4), taken(b, 16, 24), -1.0)
 
         def low(b):
             tt(B("FU", H * b, H * b + H), taken(b, 0, 8), B("VP", E * b, E * b + H), OP.add)
@@ -429,40 +427,49 @@ def rank_program(g, core, T, topo):
         def high(b):
             tt(B("X", 512 + b, 1024, 4), taken(b, 8, 16), B("VP", E * b + H, E * b + C), OP.add)
 
-        low(0)
-        quant("QB", "SB", 0, 128, "UB")
-        exchange(nxt, prv, ((B("LB", bit=dt.uint8), B("QB", bit=dt.uint8)), (B("LS"), B("SB"))), "bar", "sbar")
-        for b in range(1, 4):
-            low(b)
-        for b in range(4):
-            high(b)
+        calls = inverse(t, 1, cp)
+        calls.update({"mv": lambda x: flux(cp, x % 4, x // 4), "ms": lambda x: flux(act, x % 4, x // 4),
+                      "qm": layer, "qt": unpack, "tv": lambda x: layer_out("v", x), "ts": lambda x: layer_out("s", x),
+                      "dv": lambda x: unpack_out("v", x), "ds": lambda x: unpack_out("s", x)})
+
+        def give_back(x):
+            quant("QB", "SB", 0, 128, "UB")
+            exchange(nxt, prv, ((B("LB", bit=dt.uint8), B("QB", bit=dt.uint8)), (B("LS"), B("SB"))), "bar", "sbar")
 
         def result(a, b):
             act(B("YO", a, b), mm("QV", "SV", 0, "QX", "SX", a, b))
             sem = "outs" if a else "oute"
             dma("y", sem, T.oc[:, 4 * a:4 * b], B("QX", a, b, bit=dt.uint8))
             for k in range(4):
-                dma("s" if a == 0 and k % 2 else "y", sem, T.osc[4 * k:4 * k + 4, a:b], B("SX", a, b, p=(32 * k, 32 * k + 4)))
+                dma("y", sem, T.osc[4 * k:4 * k + 4, a:b], B("SX", a, b, p=(32 * k, 32 * k + 4)))
             dma("s", sem, T.y[:, a:b], B("YO", a, b))
 
-        if last:
-            act(B("ONR"), B("UNW", ix=B("REV")))
-            dma("y", "outs", T.on[:], (T.ONR[0:128:16, :], B("ONR")[1]))
-            quant("QX", "SX", H, C, "X")
-        back = [mm("QE", "SE", 128 * b, "LB", "LS", 0, H) for b in range(4)]
-        if last:
-            result(H, C)
-        for b in range(4):
-            tt(B("X", b, 512, 4), B("FU", H * b, H * b + H), back[b], OP.subtract)
-        if not last:
-            quant("QX", "SX", H, C, "X")
-        quant("QX", "SX", 0, H, "X")
-        if last:
-            result(0, H)
-        else:
-            send_border()
-            score(0, C)
+        def packed(x):
+            a, b = H * x, H * x + H
+            quant("QX", "SX", a, b, "X")
+            if last:
+                result(a, b)
+                return
+            if x == 0:
+                send_border()
+            score(a, b)
+            for k in range(4):
+                number(k, a, b)
+
+        def came_back(x):
             for b in range(4):
-                number(b, 0, C)
+                tt(B("X", b, 512, 4), B("FU", H * b, H * b + H), mm("QE", "SE", 128 * b, "LB", "LS", 0, H), OP.subtract)
+
+        def places_out(x):
+            if last:
+                act(B("UNN"), B("IOTA", ix=B("OFN")))
+                act(B("ONR"), B("UNN", ix=B("REV")))
+                dma("y", "outs", T.on[:], (T.ONR[0:128:16, :], B("ONR")[1]))
+
+        calls.update({"uv": lambda b: scaled("v", B("UB", b, 512, 4), taken(b, 16, 24), -1.0),
+                      "us": lambda b: scaled("s", B("UB", b, 512, 4), taken(b, 16, 24), -1.0),
+                      "qb": give_back, "lo": low, "hi": high, "qx": packed, "bk": came_back, "on": places_out})
+        for word in (LAST if last else FLUX).split():
+            play(calls, word)
     for sem in SEMAPHORES:
         wait("g", sem, count[sem])

@@ -6,18 +6,21 @@ N, R, C, H, E = 8, 3, 256, 128, 384
 CW = 1024
 PW = 272
 SEG = (0, 64, 112, 144, 160)
-EARLY = "ha co ca eq0 eq1+cb la0 la1+ta0 ta1 sc0 no sc1 ly201 pi10 bo10"
-FLUX = ("ha ms23567 mv0 co mv1 ca eq0 qm0 ts0123 cb eq1 la0 mv4 ta0 la1 qm1 ts4567 sc0 ta1 qt0 ds0123 sc1 qt1 ly2 ly01 ds45 pi1 pi0 dv67 "
-        "bo1 bo0 uv0 us2 uv1 us3 lo0 qb on lo123 hi0123 bk qx1 qx0")
-LAST = FLUX.replace("bk qx1", "qx1 bk")
+WAITS = ("no no no no  no no no no "
+         "tn0 ho0+ha0 no no  no no no no "
+         "tn1 ho1+ha1 co0+ws0 ca0  eq0+cb0 eq1 la0 no "
+         "tn2+la1+ta0 ho2+ha2+ta1 sc0 no  sc1 t20 no t00")
+FLUX = ("tn3 t10 pb0 ho3 ha3 po0 ms23567 mv0 be0 wv1 co1 mv1 gn0 ca1 eq2 qm0 ts0123 io0 cb1 eq3 la2 mv4 ta2 la3 qm1 ts4567 sc2 ta3 "
+        "qt0 ds0123 sc3 qt1 t21 t01 pb1 ds45 t11 gf3 io3 dv67 po1 us2 uv0 us3 be5 uv1 gn5 qb io5 on qv lo0123 hi0123 bk qx1 qx0")
+LAST = FLUX
 LISTS = ("float8_e4m3fn_x4 QX 384 QU 128 UQ 128 QV 128 WQ 512 QE 512 QM 256 QT 256 QB 128 LB 128",
          "uint8 SX 384 SU 128 US 128 SV 128 WS 512 SE 512 SM 256 SQ 256 SB 128 LS 128",
          "bfloat16 X 1024 UIN 512 VIN 512 ONES 520 EB 520 VP 1536 M 1024 TT 1024 DW 1088 CELL0 1024 CELL1 1024 "
-         "CELL2 1024 CELL3 1024 CELL4 1024 CELL5 1024 POS 128 CT 1536 UB 512 EE 640 DS 640 CDG 320",
-         "float32 IOTA 384 IOL 384 IOH 384 WA 768 WB 768 NAT 768 TAB 1536 SCP 384 GB 64 GA 64 GG 192 TG 768 TF 64 DD 16 "
-         "UNW 256 UNN 256 NF 16 CEA 16 CEB 16 CG 64 CM 32 FU 512 PF 32 YO 256 ONR 256",
+         "POS 128 CT 1536 UB 512 EE 640 DS 640 CDG 160",
+         "float32 IOTA 384 IOL 384 IOH 384 WA 768 WB 768 NAT 768 TAB 1536 SCP 384 GB 64 GA 32 GG 128 TG 512 TF 64 DD 16 "
+         "FI 96 ND 96 NX 384 NT 256 UNW 256 UNN 256 NF 16 CEA 16 CEB 16 CG 64 CM 32 SH 64 FU 512 PF 32 YO 256 ONR 256",
          "int32 LN 96 NI 16 T1 16 PI 8",
-         "uint16 LU 96 OF 128 OFI 2 CVC 4 NU 16 OFN 16 OFD 16 OFS 16 OFC 24 UOF 8 REV 16")
+         "uint16 LU 96 OF 128 OFI 2 CVC 4 OFN 16 OFD 16 OFS 16 OFC 24 UOF 8 REV 16")
 WIDTH = {}
 SCRATCH = {}
 for _line in LISTS:
@@ -29,7 +32,7 @@ for _i in range(8):
     WIDTH["ps%d" % _i] = 512
     SCRATCH["ps%d" % _i] = ("psum", [128, 512], "float32")
 SEMAPHORES = ["v", "s", "pe", "gp", "lx0", "lx1", "lu", "lv", "lwc", "lws", "la", "lb", "t0", "t1", "outs", "oute",
-              "brd", "bar", "sbrd", "sbar"] + ["ex%d" % _i for _i in range(8)]
+              "brd", "bar", "sbrd", "sbar"]
 
 
 def rank_program(g, core, T, topo):
@@ -202,30 +205,34 @@ def rank_program(g, core, T, topo):
     iota(pi(0), [[1, 1]], 0, 1)
     iota(B("IOTA"), [[1, E]], 0, 0)
     fill(B("ONES"), 1.0)
-    for x, (c, op) in enumerate(((7, OP.bitwise_and), (3, OP.arith_shift_right), (8, OP.bitwise_and), (16, OP.bitwise_and),
-                                 (15, OP.bitwise_and), (4, OP.bitwise_and), (64, OP.bitwise_and))):
+    for x, (c, op) in enumerate(((7, OP.bitwise_and), (64, OP.bitwise_and), (8, OP.bitwise_and), (16, OP.bitwise_and),
+                                 (15, OP.bitwise_and), (4, OP.bitwise_and), (96, OP.bitwise_and))):
         ts(pi(x + 1), pi(0), c, op)
     ts(pf(11), pi(6), -0.5, OP.mult, 1.0, OP.add)
     ts(pf(0), pi(1), 16.0, OP.mult)
-    ts(pf(3), pi(1), -32.0, OP.mult, 255.0, OP.add)
-    ts(pf(4), pi(4), -0.875, OP.mult)
+    ts(pf(3), pi(0), -2.0, OP.mult, 255.0, OP.add)
+    ts(pf(4), pi(0), -1.0, OP.mult, 255.0, OP.add)
     ts(pf(7), pi(6), -0.25, OP.mult)
     cp(pf(8), pi(5))
     cp(pf(9), pi(4))
     ts(pf(1), pi(3), 0.0, OP.is_equal, pf(11), OP.mult)
     ts(pf(2), pi(3), 0.0, OP.not_equal, pf(11), OP.mult)
     ts(B("UOF"), B("ONES", 0, 8), pf(0), OP.mult)
-    tt(pf(5), pf(3), pi(2), OP.subtract)
+    tt(pf(5), pf(3), pi(5), OP.add)
     ts(B("IOL"), B("IOTA"), pf(2), OP.mult)
     act(B("IOH"), B("IOTA"), scale=pf(1))
-    tt(pf(6), pf(5), pf(4), OP.add)
+    tt(pf(6), pf(4), pi(7), OP.subtract)
     cp(B("LU", 0, 48), B("LN", 0, 48))
     cp(B("LU", 48, 96), B("LN", 48, 96))
     quant("QX", "SX", 0, H, "X")
     send_border()
     run("g", g.affine_select, B("EB"), B("ONES"), [[-1, 520]], OP.is_equal, 0.0, 3, 4)
-    for x in range(2 * R):
-        iota(B("CELL%d" % x, 0, 768), [[0, 768]], 0, 0)
+
+    def clear_cells():
+        for z in range(2):
+            iota(B("CELL%d" % z, 0, 768), [[0, 768]], 0, 0)
+
+    clear_cells()
 
     def shifted(x):
         tt(B("WA", E * x, E * x + E), B("IOL", ix=B("LU", 48 * x + 24, 48 * x + 48)), B("IOH"), OP.add)
@@ -249,32 +256,26 @@ def rank_program(g, core, T, topo):
     act(B("US"), B("SU", ix=B("UOF")))
     for x in range(2):
         ts(B("OF", 4 + 2 * x, 6 + 2 * x), B("IOTA", 0, 2), -16.0, OP.mult, pf(5), OP.add)
-    ts(B("OFI"), B("IOTA", 0, 2), -2.0, OP.mult, pf(6), OP.add)
+    ts(B("OFI"), B("IOTA", 0, 2), -32.0, OP.mult, pf(6), OP.add)
     quant("QX", "SX", H, C, "X")
     for b in range(4):
         quant("QE", "SE", 128 * b, 128 * b + 128, "EB", 3 - b)
     score(0, C)
 
     def one(k, e, x, i):
-        return col("TG", 96 * k + 32 * x + 16 * e + 4 * (k % 4) + i)
-
-    def width(k):
-        return 96 if k % 2 else 64
+        return col("TG", 64 * k + 32 * x + 16 * e + 4 * (k % 4) + i)
 
     def look(f, k):
-        o, c, n = 2 * E * (k // 4), 96 * (k % 2), 16 * k
+        o, c, n = 2 * E * (k // 4), 64 * (k % 2), 16 * k
         f(B("GG", c, c + 32), B("TAB", o + E, o + 2 * E, ix=B("OF", n + 4, n + 6)))
-        f(B("GG", c + 32, c + width(k)), B("TAB", o, o + E, ix=B("OF", n + 6, n + 4 + width(k) // 16)))
+        f(B("GG", c + 32, c + 64), B("TAB", o, o + E, ix=B("OF", n + 6, n + 8)))
 
     def look_turn(k):
-        turn(B("TG", 96 * k, 96 * k + width(k)), B("GG", 96 * (k % 2), 96 * (k % 2) + width(k)))
+        turn(B("TG", 64 * k, 64 * k + 64), B("GG", 64 * (k % 2), 64 * (k % 2) + 64))
 
     def a_less_b(k):
         for e in range(2):
             ts(col("DD", 2 * k + e), one(k, e, 1, 1), one(k, e, 1, 0), OP.add, one(k, e, 0, 0), OP.subtract)
-
-    def list_out(k):
-        dma("y", "ex%d" % k, B("OFN", p=(16 * k, 16 * k + 16)), B("NU", 2 * k, 2 * k + 2))
 
     for x in range(2):
         cp(B("GB", 32 * x, 32 * x + 32), B("TAB", E * x, E * x + E, ix=B("OFI")))
@@ -285,10 +286,12 @@ def rank_program(g, core, T, topo):
     for e in range(2):
         ts(col("OF", 2 + e), col("TF", 16 * e), col("TF", 16 * e + 1), OP.add)
     a_less_b(0)
-    later(ts, col("CVC", 0), pi(5), 32.0, OP.mult, pf(9), OP.add)
-    later(ts, col("CVC", 2), pi(1), 32.0, OP.mult, pf(9), OP.add)
+    fill(B("FI", 0, 96, 3), 0.0)
+    fill(B("FI", 1, 96, 3), 1.0)
+    ts(col("CVC", 0), pi(5), 32.0, OP.mult, pf(9), OP.add)
+    ts(col("CVC", 2), pi(1), 32.0, OP.mult, pf(9), OP.add)
     later(ts, pf(10), pf(8), -1.0, OP.mult, 255.0, OP.add)
-    later(ts, pf(16), pi(7), 2.0, OP.mult, 1.0, OP.add)
+    later(ts, pf(16), pi(2), 2.0, OP.mult, 1.0, OP.add)
     for i in range(4):
         later(ts, pf(12 + i), pf(8), 4.0, OP.mult, 768.0 + 64 * i, OP.add)
         later(ts, B("CDG", SEG[i], SEG[i + 1]), B("IOTA", 0, 64 - 16 * i), pf(8), OP.not_equal)
@@ -297,104 +300,129 @@ def rank_program(g, core, T, topo):
     for i in range(4):
         later(ts, col("CDG", SEG[i + 1] - 1), col("CDG", SEG[i + 1] - 1), pf(12 + i), OP.mult)
     later(ts, B("POS"), B("IOTA", 0, 128), pf(16), OP.add)
-    later(cp, B("CDG", 160, 320), B("CDG", 0, 160))
     later(ts, B("REV"), B("IOTA", 0, 16), -16.0, OP.mult, pf(10), OP.add)
-    later(quant, "QV", "SV", 0, 128, "VIN")
 
-    def inverse(t, z, unwrap):
-        cell, o, p = "CELL%d" % (2 * t + z), 8 * z, (64 * z, 64 * z + 64)
+    def lists(z, p=(0, 128)):
+        return B("NT", 64 * z + 2 * z + 1, 64 * z + 64, 16, p=p)
 
-        def halves():
-            for x in range(2):
-                cp(B("OFD", o, o + 8, p=(64 * x, 64 * x + 64)), B("OFN", 8 * x, 8 * x + 8, p=p))
+    def lists_turn(z):
+        turn(B("NT", 64 * z, 64 * z + 64), B("NX", 192 * (z % 2) + 2, 192 * (z % 2) + 192, 3))
 
-        def copies():
-            unwrap(B("UNW", 128 * z, 128 * z + 128), B("IOTA", ix=B("OFD", o, o + 8)))
-            cp(B("NI", o, o + 8), B("OFD", o, o + 8))
-            cp(B("NF", o, o + 8), B("OFD", o, o + 8))
-            ts(B("CEA", o, o + 8), B("OFD", o, o + 8), pf(9), OP.add)
+    def lists_home(z):
+        for x in range(4):
+            cp(B("OFN", 4 * x, 4 * x + 4, p=(32 * z, 32 * z + 32)), lists(z, (32 * x, 32 * x + 32)))
 
-        def equal(r):
-            for i in range(4):
-                a, u = 320 * z + 160 * r, 128 * z + 64 * r
-                ts(B("EE", a + SEG[i], a + SEG[i + 1]), B("UNW", u + 16 * i, u + 64), col("NF", o + 4 * r + i), OP.is_equal)
+    def eight(buf, y):
+        return B(buf, 8 * y, 8 * y + 8)
 
-        def later_equal(r):
-            a = 320 * z + 160 * r
-            scan(B("DS", a, a + 160), B("EE", a, a + 160), B("CDG", 160 * r, 160 * r + 160), OP.max, OP.mult)
+    def lists_halves(z):
+        for x in range(4):
+            o, p = 8 * (z // 2) + 4 * (x % 2), 64 * (x // 2) + 32 * (z % 2)
+            cp(B("OFD", o, o + 4, p=(p, p + 32)), lists(z, (32 * x, 32 * x + 32)))
 
-        def target(r):
-            for i in range(4):
-                c = o + 4 * r + i
-                ts(col("OFS", c), col("DS", 320 * z + 160 * r + SEG[i + 1] - 1), col("CEB", c), OP.max)
+    def copies(y):
+        cp(eight("NI", y), eight("OFD", y))
+        cp(eight("NF", y), eight("OFD", y))
+        ts(eight("CEA", y), eight("OFD", y), pf(9), OP.add)
 
-        def scatter(r):
-            cp(B(cell, ix=B("OFS", o + 4 * r, o + 4 * r + 4)), B("POS", 64 * r, 64 * r + 64))
+    def unwrap(f, y):
+        f(B("UNW", 128 * y, 128 * y + 128), B("IOTA", ix=eight("OFD", y)))
 
-        def lay(x):
-            turn(B("CT", 768 * z + 256 * x, 768 * z + 256 * x + 256), B(cell, 256 * x, 256 * x + 256))
+    def equal(r):
+        for i in range(4):
+            ts(B("EE", 160 * r + SEG[i], 160 * r + SEG[i + 1]), B("UNW", 64 * r + 16 * i, 64 * r + 64), col("NF", 4 * r + i), OP.is_equal)
 
-        def pick(x):
-            a = 768 * z + 512 * x
-            cp(B("CG", 32 * z + 16 * x, 32 * z + 16 * x + 16), B("CT", a, a + 512 - 256 * x, ix=B("CVC", 2 * x, 2 * x + 1)))
+    def later_equal(r):
+        scan(B("DS", 160 * r, 160 * r + 160), B("EE", 160 * r, 160 * r + 160), B("CDG"), OP.max, OP.mult)
 
-        def both(x):
-            a, n = 32 * z + 16 * x, 16 - 8 * x
-            tt(B("CM", 16 * x, 16 * x + n, p=p), B("CG", a, a + n, p=(0, 64)), B("CG", a, a + n, p=(64, 128)), OP.max)
+    def target(r):
+        for i in range(4):
+            ts(col("OFS", 4 * r + i), col("DS", 160 * r + SEG[i + 1] - 1), col("CEB", 4 * r + i), OP.max)
+
+    def scatter(r):
+        cp(B("CELL%d" % (r // 2), ix=B("OFS", 4 * r, 4 * r + 4)), B("POS", 64 * (r % 2), 64 * (r % 2) + 64))
+
+    def lay(y, x):
+        turn(B("CT", 768 * y + 256 * x, 768 * y + 256 * x + 256), B("CELL%d" % y, 256 * x, 256 * x + 256))
+
+    def pick(f, y, x):
+        a = 768 * y + 512 * x
+        f(B("CG", 32 * y + 16 * x, 32 * y + 16 * x + 16), B("CT", a, a + 512 - 256 * x, ix=B("CVC", 2 * x, 2 * x + 1)))
+
+    def part(x):
+        a, b = ((0, 24), (16, 24), (0, 16))[x // 2]
+        return a, b, 32 * (x % 2), (64 * (x % 2), 64 * (x % 2) + 64)
+
+    def beside(x):
+        a, b, o, p = part(x)
+        cp(B("SH", o + a, o + b, p=(0, 64)), B("CG", o + a, o + b, p=(64, 128)))
+
+    def greater(x, near):
+        a, b, o, p = part(x)
+        tt(B("CM", a, b, p=p), B("CG", o + a, o + b, p=(0, 64)), B("SH", o + a, o + b, p=(0, 64)) if near else B("CG", o + a, o + b, p=(64, 128)), OP.max)
+        if not near:
             wait("v", "v", count["v"])
-            cp(B("OFC", 16 * x, 16 * x + n, p=p), B("CM", 16 * x, 16 * x + n, p=p))
 
-        return {"ha": lambda x: halves(), "co": lambda x: copies(), "eq": equal, "la": later_equal, "ta": target, "sc": scatter,
-                "ca": lambda x: ts(B("T1", o, o + 8), B("NI", o, o + 8), 0x1F0, OP.bitwise_and),
-                "cb": lambda x: tt(B("CEB", o, o + 8), B("CEA", o, o + 8), B("T1", o, o + 8), OP.add),
-                "ly": lay, "pi": pick, "bo": both, "no": lambda x: None}
+    def inverse_out(x):
+        a, b, o, p = part(x)
+        cp(B("OFC", a, b, p=p), B("CM", a, b, p=p))
 
-    def play(calls, word):
+    calls = {"tn": lists_turn, "ho": lists_home, "ha": lists_halves, "co": copies, "wv": lambda y: unwrap(cp, y), "ws": lambda y: unwrap(act, y),
+             "ca": lambda y: ts(eight("T1", y), eight("NI", y), 0x1F0, OP.bitwise_and),
+             "cb": lambda y: tt(eight("CEB", y), eight("CEA", y), eight("T1", y), OP.add),
+             "eq": equal, "la": later_equal, "ta": target, "sc": scatter,
+             "t0": lambda y: lay(y, 0), "t1": lambda y: lay(y, 1), "t2": lambda y: lay(y, 2),
+             "po": lambda y: pick(cp, y, 0), "pb": lambda y: pick(cp, y, 1), "be": beside, "gn": lambda x: greater(x, True),
+             "gf": lambda x: greater(x, False), "io": inverse_out, "no": lambda z: spare(3)}
+
+    def play(word):
         for name in word.split("+"):
             for x in name[2:] or "0":
-                calls[name[:2]](int(x))
+                calls[name[:2]](int(x, 16))
 
     for t in range(R):
         last = t == R - 1
         score(C, E)
+        waits = WAITS.split()
         for k in range(8):
-            n, c = 16 * k, 32 * (k % 2)
-            if k == 5:
-                spare(99)
-                early = inverse(t, 0, act)
-                for word in EARLY.split():
-                    later(play, early, word)
+            n, c, x0 = 16 * k, 32 * (k % 2), 192 * (k // 2 % 2)
+            flags = B("FI", 2, 96, 3) if k % 2 else B("GA")
 
             def choose(out, d, e, y):
                 ts(out, d, col("TF", c + 16 * e + k), OP.mult, y, OP.add)
 
             cp(B("GB", c, c + 32), B("SCP", ix=B("OF", n, n + 2)))
-            if k:
+            if 0 < k < 7:
                 look(act, k)
-            if k < 4:
-                number(k, C if t else 0, E)
-            spare(2 if k < 5 else 1)
-            tt(B("GA", c, c + 32), B("SCP", ix=B("OF", n + 2, n + 4)), B("GB", c, c + 32), OP.is_le)
-            if k:
-                look_turn(k)
-            spare()
-            turn(B("TF", c, c + 32), B("GA", c, c + 32))
-            if k:
-                a_less_b(k)
             if k % 2:
-                cp(B("NU", 2 * k - 2, 2 * k), B("TG", 96 * k + 64, 96 * k + 96, 16))
-                list_out(k - 1)
-            spare()
+                act(B("ND", 0, 96, 3), B("IOTA", ix=B("OF", n + 2, n + 4)))
+                act(B("ND", 1, 96, 3), B("IOTA", ix=B("OF", n, n + 2)), scale=-1.0)
+                act(B("ND", 2, 96, 3), B("IOTA", ix=B("OF", n, n + 2)))
+                for w in range(2):
+                    act(B("NX", x0 + 96 * w + 2, x0 + 96 * w + 48, 3), B("IOTA", ix=col("OF", n + 8 + 2 * w)))
+            elif k < 7:
+                number(k // 2, C if t else 0, E)
+            play(waits.pop(0))
+            tt(flags, B("SCP", ix=B("OF", n + 2, n + 4)), B("GB", c, c + 32), OP.is_le)
+            if 0 < k < 7:
+                look_turn(k)
+            play(waits.pop(0))
+            if k < 7:
+                turn(B("TF", c, c + 32), flags)
+            if k in (2, 4, 6):
+                a_less_b(k)
+            play(waits.pop(0))
             if k < 7:
                 for x, i, o in ((0, 2, 16), (0, 0, 20), (1, 0, 22), (1, 2, 18)):
-                    for e in range(2):
+                    for e in range(2 if k < 6 or i else 0):
                         choose(col("OF", n + o + e), one(k, e, x, i + 1), e, one(k, e, x, i))
-            for e in range(2):
-                choose(col("NU", 2 * k + e) if k % 2 else col("OF", n + 24 + e), col("DD", 2 * k + e), e, one(k, e, 0, 0))
             if k % 2:
-                list_out(k)
-            spare()
-        spare(99)
+                for w in range(2):
+                    scan(B("NX", x0 + 96 * w + 48, x0 + 96 * w + 96), B("FI", 48 * w, 48 * w + 48), B("ND", 48 * w, 48 * w + 48), OP.mult, OP.add)
+            else:
+                for e in range(2):
+                    choose(col("OF", n + 24 + 2 * e), col("DD", 2 * k + e), e, one(k, e, 0, 0))
+            play(waits.pop(0))
 
         def flux(f, b, x):
             f(B("M", 512 * x + b, 512 * x + 512, 4), B("VP", E * b, E * b + E, ix=B("OFN", 8 * x, 8 * x + 8)))
@@ -427,7 +455,6 @@ def rank_program(g, core, T, topo):
         def high(b):
             tt(B("X", 512 + b, 1024, 4), taken(b, 8, 16), B("VP", E * b + H, E * b + C), OP.add)
 
-        calls = inverse(t, 1, cp)
         calls.update({"mv": lambda x: flux(cp, x % 4, x // 4), "ms": lambda x: flux(act, x % 4, x // 4),
                       "qm": layer, "qt": unpack, "tv": lambda x: layer_out("v", x), "ts": lambda x: layer_out("s", x),
                       "dv": lambda x: unpack_out("v", x), "ds": lambda x: unpack_out("s", x)})
@@ -452,6 +479,7 @@ def rank_program(g, core, T, topo):
                 return
             if x == 0:
                 send_border()
+                clear_cells()
             score(a, b)
             for k in range(4):
                 number(k, a, b)
@@ -468,8 +496,8 @@ def rank_program(g, core, T, topo):
 
         calls.update({"uv": lambda b: scaled("v", B("UB", b, 512, 4), taken(b, 16, 24), -1.0),
                       "us": lambda b: scaled("s", B("UB", b, 512, 4), taken(b, 16, 24), -1.0),
-                      "qb": give_back, "lo": low, "hi": high, "qx": packed, "bk": came_back, "on": places_out})
+                      "qv": lambda x: quant("QV", "SV", 0, 128, "VIN") if t == 0 else None, "qb": give_back, "lo": low, "hi": high, "qx": packed, "bk": came_back, "on": places_out})
         for word in (LAST if last else FLUX).split():
-            play(calls, word)
+            play(word)
     for sem in SEMAPHORES:
         wait("g", sem, count[sem])

from concourse.mybir import dt, AluOpType, ActivationFunctionType

OP = AluOpType
AF = ActivationFunctionType
N, R, C, H, E = 8, 3, 256, 128, 384
CW = 1024
PW = 272
SEG = (0, 64, 112, 144, 160)
WAITS = ("no no no no  no no no no "
         "tn0 ho0+ha0 no no  no no no no "
         "tn1 ho1+ha1 co0+ws0 ca0  eq0+cb0 eq1 la0 no "
         "tn2+la1+ta0 ho2+ha2+ta1 sc0 no  sc1 t20 no t00")
FLUX = ("tn3 t10 pb0 ho3 ha3 po0 ms23567 mv0 be0 wv1 co1 mv1 gn0 ca1 eq2 qm0 ts0123 io0 cb1 eq3 la2 mv4 ta2 la3 qm1 ts4567 sc2 ta3 "
        "qt0 ds0123 sc3 qt1 t21 t01 pb1 ds45 t11 gf3 io3 dv67 po1 us2 uv0 us3 be5 uv1 gn5 qb io5 on qv lo0123 hi0123 bk qx1 qx0")
LAST = FLUX
LISTS = ("float8_e4m3fn_x4 QX 384 QU 128 UQ 128 QV 128 WQ 512 QE 512 QM 256 QT 256 QB 128 LB 128",
         "uint8 SX 384 SU 128 US 128 SV 128 WS 512 SE 512 SM 256 SQ 256 SB 128 LS 128",
         "bfloat16 X 1024 UIN 512 VIN 512 ONES 520 EB 520 VP 1536 M 1024 TT 1024 DW 1088 CELL0 1024 CELL1 1024 "
         "POS 128 CT 1536 UB 512 EE 640 DS 640 CDG 160",
         "float32 IOTA 384 IOL 384 IOH 384 WA 768 WB 768 NAT 768 TAB 1536 SCP 384 GB 64 GA 32 GG 128 TG 512 TF 64 DD 16 "
         "FI 96 ND 96 NX 384 NT 256 UNW 256 UNN 256 NF 16 CEA 16 CEB 16 CG 64 CM 32 SH 64 FU 512 PF 32 YO 256 ONR 256",
         "int32 LN 96 NI 16 T1 16 PI 8",
         "uint16 LU 96 OF 128 OFI 2 CVC 4 OFN 16 OFD 16 OFS 16 OFC 24 UOF 8 REV 16")
WIDTH = {}
SCRATCH = {}
for _line in LISTS:
    _w = _line.split()
    for _i in range(1, len(_w), 2):
        WIDTH[_w[_i]] = int(_w[_i + 1])
        SCRATCH[_w[_i]] = ("sbuf", [128, int(_w[_i + 1])], _w[0])
for _i in range(8):
    WIDTH["ps%d" % _i] = 512
    SCRATCH["ps%d" % _i] = ("psum", [128, 512], "float32")
SEMAPHORES = ["v", "s", "pe", "gp", "lx0", "lx1", "lu", "lv", "lwc", "lws", "la", "lb", "t0", "t1", "outs", "oute",
              "brd", "bar", "sbrd", "sbar"]


def rank_program(g, core, T, topo):
    rank = T.rank_of(core)
    if rank is None:
        return
    nxt, prv = T.cores[(rank + 1) % N], T.cores[(rank - 1) % N]
    v, s = g.vector, g.scalar
    eng = {"pe": g.tensor, "v": v, "s": s, "g": g, "y": g.sync}
    home = {"pe": "pe", "v": "v", "s": "s", "g": "gp"}
    count = {k: 0 for k in SEMAPHORES}
    held = {}
    log = {}

    def B(n, a=0, b=None, st=1, ix=None, bit=None, p=(0, 128)):
        b = WIDTH[n] if b is None else b
        ap = T[n][p[0]:p[1], a:b] if st == 1 else T[n][p[0]:p[1], a:b:st]
        if bit:
            ap = ap.bitcast(bit)
        if ix:
            ap = ap.indirect(ix[0])
        return (ap, [(n, p[0], p[1], a, b, st)], ix[1] if ix else [])

    def wait(q, sem, val):
        if held.get((q, sem), 0) < val:
            held[(q, sem)] = val
            eng[q].wait_ge(T.sem[sem], val)

    def order(q, reads, writes):
        need = {}
        for kinds, regs in (("wW", reads), ("rw", writes)):
            for n, p0, p1, c0, c1, st in regs:
                for k, a0, a1, b0, b1, su, sem, val, far in log.get(n, ()):
                    if k in kinds and a0 < p1 and p0 < a1 and b0 < c1 and c0 < b1 and (st != su or (c0 - b0) % st == 0):
                        need[sem] = max(need.get(sem, 0), count[sem] if far else val)
        for sem in need:
            wait(q, sem, need[sem])

    def note(reads, writes, sem, far):
        for n, p0, p1, c0, c1, st in writes:
            log[n] = [x for x in log.get(n, ()) if not (p0 <= x[1] and x[2] <= p1 and c0 <= x[3] and x[4] <= c1
                                                        and (st == 1 or st == x[5] and (c0 - x[3]) % st == 0))]
        for n, p0, p1, c0, c1, st in reads:
            if st == 1:
                log[n] = [("W",) + x[1:] if x[0] == "w" and p0 <= x[1] and x[2] <= p1 and c0 <= x[3] and x[4] <= c1 else x
                          for x in log.get(n, ())]
        for kind, regs in (("w", writes), ("r", reads)):
            for r in regs:
                log.setdefault(r[0], []).append((kind,) + r[1:] + (sem, count[sem], far))

    def run(q, call, *args, outs=1, more=(), **kw):
        reads, writes, real = list(more), [], []
        for i, x in enumerate(args):
            if isinstance(x, tuple):
                (writes if i < outs else reads).extend(x[1])
                reads.extend(x[2])
                x = x[0]
            real.append(x)
        order(q, reads, writes)
        call(*real, **kw).then_inc(T.sem[home[q]], 1)
        count[home[q]] += 1
        note(reads, writes, home[q], False)

    def dma(q, sem, out, in_):
        w, r = (out[1] if isinstance(out, tuple) else []), (in_[1] if isinstance(in_, tuple) else [])
        order(q, r, w)
        eng[q].dma_start(out[0] if isinstance(out, tuple) else out, in_[0] if isinstance(in_, tuple) else in_).then_inc(T.sem[sem], 16)
        count[sem] += 16
        note(r, w, sem, True)

    def engines(a, b):
        return topo.engines(a, b)[:8]

    def exchange(dst, src, pairs, remote, local):
        reads = [r for o, i in pairs for r in i[1]]
        order("g", reads, [])
        rid, pid, _ = topo.addr(dst)
        es = engines(core, dst)
        for o, i in pairs:
            g.remote_dma(out_ap=o[0], in_ap=i[0], remote_sem=T.sem[remote], local_sem=T.sem[local], pid=pid, routing_id=rid,
                         dma_engine_mask=sum(1 << e for e in es))
            count[local] += len(es)
        note(reads, [], local, True)
        count[remote] += len(pairs) * len(engines(src, core))
        note([], [r for o, i in pairs for r in o[1]], remote, True)

    def ts(out, in0, s1, op0, s2=None, op1=None):
        run("v", v.tensor_scalar, out, in0, s1, s2, op0, *((op1,) if op1 else ()))

    def tt(out, in0, in1, op):
        run("v", v.tensor_tensor, out, in0, in1, op)

    def cp(out, in_):
        run("v", v.tensor_copy, out, in_)

    def act(out, in_, func=AF.Copy, **kw):
        if isinstance(kw.get("scale"), tuple):
            run("s", s.activation, out, in_, func, more=kw["scale"][1], scale=kw["scale"][0])
        else:
            run("s", s.activation, out, in_, func, **kw)

    def scaled(q, out, in_, c):
        if q == "v":
            ts(out, in_, c, OP.mult)
        else:
            act(out, in_, scale=c)

    def scan(out, d0, d1, op0, op1):
        run("v", v.tensor_tensor_scan, out, d0, d1, 0.0, op0, op1)

    def turn(out, in_):
        run("v", v.transpose, out, in_)

    def fill(x, c):
        run("v", v.memset, x, c)

    def iota(out, pattern, base, cm):
        run("g", g.iota, out, pattern, base, cm, allow_small_or_imprecise_dtypes=True)

    def quant(q, sc, a, b, tile, o=None):
        o = 4 * a if o is None else o
        run("v", v.quantize_mx, B(q, a, b), B(sc, a, b), B(tile, o, o + 4 * (b - a)), outs=2)

    bank = [0]

    def mm(lq, ls, la, rq, rs, a, b):
        p = "ps%d" % (bank[0] % 8)
        bank[0] += 1
        run("pe", g.tensor.matmul_mx, B(p, 0, b - a), B(lq, la, la + 128), B(ls, la, la + 128), B(rq, a, b), B(rs, a, b), True, True)
        return B(p, 0, b - a)

    def score(a, b):
        act(B("SCP", a, b), mm("UQ", "US", 0, "QX", "SX", a, b), AF.Abs)

    def number(k, a, b):
        act(B("VP", E * k + a, E * k + b), mm("QE", "SE", 128 * k, "QX", "SX", a, b))

    def send_border():
        exchange(prv, nxt, ((B("QX", C, E, bit=dt.uint8), B("QX", 0, H, bit=dt.uint8)), (B("SX", C, E), B("SX", 0, H))), "brd", "sbrd")

    todo = []

    def later(f, *a):
        todo.append(lambda: f(*a))

    def spare(n=1):
        for _ in range(n):
            if todo:
                todo.pop(0)()

    def col(buf, x):
        return B(buf, x, x + 1)

    def pi(x):
        return col("PI", x)

    def pf(x):
        return col("PF", x)

    dma("y", "lx0", B("X", 0, 512), T.x[:, 0:512])
    for q, sem, x, src in (("s", "la", 0, T.lf), ("y", "lb", 1, T.rt)):
        dma(q, sem, B("LN", 48 * x, 48 * x + 24), src[:])
        dma(q, sem, B("LN", 48 * x + 24, 48 * x + 48, p=(0, 112)), src[16:128, :])
        dma(q, sem, B("LN", 48 * x + 24, 48 * x + 48, p=(112, 128)), src[0:16, :])
    dma("s", "lu", B("UIN"), T.u[:])
    dma("y", "lx1", B("X", 512, 1024), T.x[:, 512:1024])
    dma("y", "lwc", B("WQ", bit=dt.uint8), T.wc[:])
    dma("y", "lws", B("WS"), T.ws[:])
    dma("y", "lv", B("VIN"), T.v[:])
    iota(pi(0), [[1, 1]], 0, 1)
    iota(B("IOTA"), [[1, E]], 0, 0)
    fill(B("ONES"), 1.0)
    for x, (c, op) in enumerate(((7, OP.bitwise_and), (64, OP.bitwise_and), (8, OP.bitwise_and), (16, OP.bitwise_and),
                                 (15, OP.bitwise_and), (4, OP.bitwise_and), (96, OP.bitwise_and))):
        ts(pi(x + 1), pi(0), c, op)
    ts(pf(11), pi(6), -0.5, OP.mult, 1.0, OP.add)
    ts(pf(0), pi(1), 16.0, OP.mult)
    ts(pf(3), pi(0), -2.0, OP.mult, 255.0, OP.add)
    ts(pf(4), pi(0), -1.0, OP.mult, 255.0, OP.add)
    ts(pf(7), pi(6), -0.25, OP.mult)
    cp(pf(8), pi(5))
    cp(pf(9), pi(4))
    ts(pf(1), pi(3), 0.0, OP.is_equal, pf(11), OP.mult)
    ts(pf(2), pi(3), 0.0, OP.not_equal, pf(11), OP.mult)
    ts(B("UOF"), B("ONES", 0, 8), pf(0), OP.mult)
    tt(pf(5), pf(3), pi(5), OP.add)
    ts(B("IOL"), B("IOTA"), pf(2), OP.mult)
    act(B("IOH"), B("IOTA"), scale=pf(1))
    tt(pf(6), pf(4), pi(7), OP.subtract)
    cp(B("LU", 0, 48), B("LN", 0, 48))
    cp(B("LU", 48, 96), B("LN", 48, 96))
    quant("QX", "SX", 0, H, "X")
    send_border()
    run("g", g.affine_select, B("EB"), B("ONES"), [[-1, 520]], OP.is_equal, 0.0, 3, 4)

    def clear_cells():
        for z in range(2):
            iota(B("CELL%d" % z, 0, 768), [[0, 768]], 0, 0)

    clear_cells()

    def shifted(x):
        tt(B("WA", E * x, E * x + E), B("IOL", ix=B("LU", 48 * x + 24, 48 * x + 48)), B("IOH"), OP.add)
        act(B("WB", E * x, E * x + E), B("WA", E * x, E * x + E), scale=pf(7))

    def tables(x):
        a, b = ("WA", "WB") if x else ("WB", "WA")
        tt(B("NAT", E * x, E * x + E), B(a, E * x, E * x + E, ix=B("LU", 48 * x, 48 * x + 24)), B(b, E * x, E * x + E), OP.add)

    shifted(0)
    shifted(1)
    quant("QU", "SU", 0, 128, "UIN")
    tables(0)
    tables(1)
    for x in range(2):
        for h in range(8):
            o = 64 * x + h % 4
            dma("s" if x == 0 and h % 2 else "y", "t%d" % x, B("TAB", 2 * E * x, 2 * E * x + 2 * E, p=(16 * h, 16 * h + 16)),
                (T.NAT[o:o + 61:4, :], B("NAT")[1]))
    cp(B("UQ", bit=dt.uint32), B("QU", bit=dt.uint32, ix=B("UOF")))
    act(B("US"), B("SU", ix=B("UOF")))
    for x in range(2):
        ts(B("OF", 4 + 2 * x, 6 + 2 * x), B("IOTA", 0, 2), -16.0, OP.mult, pf(5), OP.add)
    ts(B("OFI"), B("IOTA", 0, 2), -32.0, OP.mult, pf(6), OP.add)
    quant("QX", "SX", H, C, "X")
    for b in range(4):
        quant("QE", "SE", 128 * b, 128 * b + 128, "EB", 3 - b)
    score(0, C)

    def one(k, e, x, i):
        return col("TG", 64 * k + 32 * x + 16 * e + 4 * (k % 4) + i)

    def look(f, k):
        o, c, n = 2 * E * (k // 4), 64 * (k % 2), 16 * k
        f(B("GG", c, c + 32), B("TAB", o + E, o + 2 * E, ix=B("OF", n + 4, n + 6)))
        f(B("GG", c + 32, c + 64), B("TAB", o, o + E, ix=B("OF", n + 6, n + 8)))

    def look_turn(k):
        turn(B("TG", 64 * k, 64 * k + 64), B("GG", 64 * (k % 2), 64 * (k % 2) + 64))

    def a_less_b(k):
        for e in range(2):
            ts(col("DD", 2 * k + e), one(k, e, 1, 1), one(k, e, 1, 0), OP.add, one(k, e, 0, 0), OP.subtract)

    for x in range(2):
        cp(B("GB", 32 * x, 32 * x + 32), B("TAB", E * x, E * x + E, ix=B("OFI")))
    look(act, 0)
    turn(B("TF"), B("GB"))
    look_turn(0)
    cp(B("OF", 0, 2), B("TF", 32, 64, 16))
    for e in range(2):
        ts(col("OF", 2 + e), col("TF", 16 * e), col("TF", 16 * e + 1), OP.add)
    a_less_b(0)
    fill(B("FI", 0, 96, 3), 0.0)
    fill(B("FI", 1, 96, 3), 1.0)
    ts(col("CVC", 0), pi(5), 32.0, OP.mult, pf(9), OP.add)
    ts(col("CVC", 2), pi(1), 32.0, OP.mult, pf(9), OP.add)
    later(ts, pf(10), pf(8), -1.0, OP.mult, 255.0, OP.add)
    later(ts, pf(16), pi(2), 2.0, OP.mult, 1.0, OP.add)
    for i in range(4):
        later(ts, pf(12 + i), pf(8), 4.0, OP.mult, 768.0 + 64 * i, OP.add)
        later(ts, B("CDG", SEG[i], SEG[i + 1]), B("IOTA", 0, 64 - 16 * i), pf(8), OP.not_equal)
    for b in range(4):
        later(fill, col("DW", PW * b), 0.0)
    for i in range(4):
        later(ts, col("CDG", SEG[i + 1] - 1), col("CDG", SEG[i + 1] - 1), pf(12 + i), OP.mult)
    later(ts, B("POS"), B("IOTA", 0, 128), pf(16), OP.add)
    later(ts, B("REV"), B("IOTA", 0, 16), -16.0, OP.mult, pf(10), OP.add)

    def lists(z, p=(0, 128)):
        return B("NT", 64 * z + 2 * z + 1, 64 * z + 64, 16, p=p)

    def lists_turn(z):
        turn(B("NT", 64 * z, 64 * z + 64), B("NX", 192 * (z % 2) + 2, 192 * (z % 2) + 192, 3))

    def lists_home(z):
        for x in range(4):
            cp(B("OFN", 4 * x, 4 * x + 4, p=(32 * z, 32 * z + 32)), lists(z, (32 * x, 32 * x + 32)))

    def eight(buf, y):
        return B(buf, 8 * y, 8 * y + 8)

    def lists_halves(z):
        for x in range(4):
            o, p = 8 * (z // 2) + 4 * (x % 2), 64 * (x // 2) + 32 * (z % 2)
            cp(B("OFD", o, o + 4, p=(p, p + 32)), lists(z, (32 * x, 32 * x + 32)))

    def copies(y):
        cp(eight("NI", y), eight("OFD", y))
        cp(eight("NF", y), eight("OFD", y))
        ts(eight("CEA", y), eight("OFD", y), pf(9), OP.add)

    def unwrap(f, y):
        f(B("UNW", 128 * y, 128 * y + 128), B("IOTA", ix=eight("OFD", y)))

    def equal(r):
        for i in range(4):
            ts(B("EE", 160 * r + SEG[i], 160 * r + SEG[i + 1]), B("UNW", 64 * r + 16 * i, 64 * r + 64), col("NF", 4 * r + i), OP.is_equal)

    def later_equal(r):
        scan(B("DS", 160 * r, 160 * r + 160), B("EE", 160 * r, 160 * r + 160), B("CDG"), OP.max, OP.mult)

    def target(r):
        for i in range(4):
            ts(col("OFS", 4 * r + i), col("DS", 160 * r + SEG[i + 1] - 1), col("CEB", 4 * r + i), OP.max)

    def scatter(r):
        cp(B("CELL%d" % (r // 2), ix=B("OFS", 4 * r, 4 * r + 4)), B("POS", 64 * (r % 2), 64 * (r % 2) + 64))

    def lay(y, x):
        turn(B("CT", 768 * y + 256 * x, 768 * y + 256 * x + 256), B("CELL%d" % y, 256 * x, 256 * x + 256))

    def pick(f, y, x):
        a = 768 * y + 512 * x
        f(B("CG", 32 * y + 16 * x, 32 * y + 16 * x + 16), B("CT", a, a + 512 - 256 * x, ix=B("CVC", 2 * x, 2 * x + 1)))

    def part(x):
        a, b = ((0, 24), (16, 24), (0, 16))[x // 2]
        return a, b, 32 * (x % 2), (64 * (x % 2), 64 * (x % 2) + 64)

    def beside(x):
        a, b, o, p = part(x)
        cp(B("SH", o + a, o + b, p=(0, 64)), B("CG", o + a, o + b, p=(64, 128)))

    def greater(x, near):
        a, b, o, p = part(x)
        tt(B("CM", a, b, p=p), B("CG", o + a, o + b, p=(0, 64)), B("SH", o + a, o + b, p=(0, 64)) if near else B("CG", o + a, o + b, p=(64, 128)), OP.max)
        if not near:
            wait("v", "v", count["v"])

    def inverse_out(x):
        a, b, o, p = part(x)
        cp(B("OFC", a, b, p=p), B("CM", a, b, p=p))

    calls = {"tn": lists_turn, "ho": lists_home, "ha": lists_halves, "co": copies, "wv": lambda y: unwrap(cp, y), "ws": lambda y: unwrap(act, y),
             "ca": lambda y: ts(eight("T1", y), eight("NI", y), 0x1F0, OP.bitwise_and),
             "cb": lambda y: tt(eight("CEB", y), eight("CEA", y), eight("T1", y), OP.add),
             "eq": equal, "la": later_equal, "ta": target, "sc": scatter,
             "t0": lambda y: lay(y, 0), "t1": lambda y: lay(y, 1), "t2": lambda y: lay(y, 2),
             "po": lambda y: pick(cp, y, 0), "pb": lambda y: pick(cp, y, 1), "be": beside, "gn": lambda x: greater(x, True),
             "gf": lambda x: greater(x, False), "io": inverse_out, "no": lambda z: spare(3)}

    def play(word):
        for name in word.split("+"):
            for x in name[2:] or "0":
                calls[name[:2]](int(x, 16))

    for t in range(R):
        last = t == R - 1
        score(C, E)
        waits = WAITS.split()
        for k in range(8):
            n, c, x0 = 16 * k, 32 * (k % 2), 192 * (k // 2 % 2)
            flags = B("FI", 2, 96, 3) if k % 2 else B("GA")

            def choose(out, d, e, y):
                ts(out, d, col("TF", c + 16 * e + k), OP.mult, y, OP.add)

            cp(B("GB", c, c + 32), B("SCP", ix=B("OF", n, n + 2)))
            if 0 < k < 7:
                look(act, k)
            if k % 2:
                act(B("ND", 0, 96, 3), B("IOTA", ix=B("OF", n + 2, n + 4)))
                act(B("ND", 1, 96, 3), B("IOTA", ix=B("OF", n, n + 2)), scale=-1.0)
                act(B("ND", 2, 96, 3), B("IOTA", ix=B("OF", n, n + 2)))
                for w in range(2):
                    act(B("NX", x0 + 96 * w + 2, x0 + 96 * w + 48, 3), B("IOTA", ix=col("OF", n + 8 + 2 * w)))
            elif k < 7:
                number(k // 2, C if t else 0, E)
            play(waits.pop(0))
            tt(flags, B("SCP", ix=B("OF", n + 2, n + 4)), B("GB", c, c + 32), OP.is_le)
            if 0 < k < 7:
                look_turn(k)
            play(waits.pop(0))
            if k < 7:
                turn(B("TF", c, c + 32), flags)
            if k in (2, 4, 6):
                a_less_b(k)
            play(waits.pop(0))
            if k < 7:
                for x, i, o in ((0, 2, 16), (0, 0, 20), (1, 0, 22), (1, 2, 18)):
                    for e in range(2 if k < 6 or i else 0):
                        choose(col("OF", n + o + e), one(k, e, x, i + 1), e, one(k, e, x, i))
            if k % 2:
                for w in range(2):
                    scan(B("NX", x0 + 96 * w + 48, x0 + 96 * w + 96), B("FI", 48 * w, 48 * w + 48), B("ND", 48 * w, 48 * w + 48), OP.mult, OP.add)
            else:
                for e in range(2):
                    choose(col("OF", n + 24 + 2 * e), col("DD", 2 * k + e), e, one(k, e, 0, 0))
            play(waits.pop(0))

        def flux(f, b, x):
            f(B("M", 512 * x + b, 512 * x + 512, 4), B("VP", E * b, E * b + E, ix=B("OFN", 8 * x, 8 * x + 8)))

        made = {}

        def layer(x):
            quant("QM", "SM", H * x, H * x + H, "M")
            for b in range(4):
                made["t", 4 * x + b] = mm("WQ", "WS", 128 * b, "QM", "SM", H * x, H * x + H)

        def unpack(x):
            quant("QT", "SQ", H * x, H * x + H, "TT")
            for b in range(4):
                made["d", 4 * x + b] = mm("QE", "SE", 128 * b, "QT", "SQ", H * x, H * x + H)

        def layer_out(q, x):
            scaled(q, B("TT", 512 * (x // 4) + x % 4, 512 * (x // 4) + 512, 4), made["t", x], 0.03125)

        def unpack_out(q, x):
            o = PW * (x % 4) + 1 + H * (x // 4)
            scaled(q, B("DW", o, o + H), made["d", x], -1.0)

        def taken(b, w0, w1):
            return B("DW", PW * b, PW * b + 257, ix=B("OFC", w0, w1))

        def low(b):
            tt(B("FU", H * b, H * b + H), taken(b, 0, 8), B("VP", E * b, E * b + H), OP.add)

        def high(b):
            tt(B("X", 512 + b, 1024, 4), taken(b, 8, 16), B("VP", E * b + H, E * b + C), OP.add)

        calls.update({"mv": lambda x: flux(cp, x % 4, x // 4), "ms": lambda x: flux(act, x % 4, x // 4),
                      "qm": layer, "qt": unpack, "tv": lambda x: layer_out("v", x), "ts": lambda x: layer_out("s", x),
                      "dv": lambda x: unpack_out("v", x), "ds": lambda x: unpack_out("s", x)})

        def give_back(x):
            quant("QB", "SB", 0, 128, "UB")
            exchange(nxt, prv, ((B("LB", bit=dt.uint8), B("QB", bit=dt.uint8)), (B("LS"), B("SB"))), "bar", "sbar")

        def result(a, b):
            act(B("YO", a, b), mm("QV", "SV", 0, "QX", "SX", a, b))
            sem = "outs" if a else "oute"
            dma("y", sem, T.oc[:, 4 * a:4 * b], B("QX", a, b, bit=dt.uint8))
            for k in range(4):
                dma("y", sem, T.osc[4 * k:4 * k + 4, a:b], B("SX", a, b, p=(32 * k, 32 * k + 4)))
            dma("s", sem, T.y[:, a:b], B("YO", a, b))

        def packed(x):
            a, b = H * x, H * x + H
            quant("QX", "SX", a, b, "X")
            if last:
                result(a, b)
                return
            if x == 0:
                send_border()
                clear_cells()
            score(a, b)
            for k in range(4):
                number(k, a, b)

        def came_back(x):
            for b in range(4):
                tt(B("X", b, 512, 4), B("FU", H * b, H * b + H), mm("QE", "SE", 128 * b, "LB", "LS", 0, H), OP.subtract)

        def places_out(x):
            if last:
                act(B("UNN"), B("IOTA", ix=B("OFN")))
                act(B("ONR"), B("UNN", ix=B("REV")))
                dma("y", "outs", T.on[:], (T.ONR[0:128:16, :], B("ONR")[1]))

        calls.update({"uv": lambda b: scaled("v", B("UB", b, 512, 4), taken(b, 16, 24), -1.0),
                      "us": lambda b: scaled("s", B("UB", b, 512, 4), taken(b, 16, 24), -1.0),
                      "qv": lambda x: quant("QV", "SV", 0, 128, "VIN") if t == 0 else None, "qb": give_back, "lo": low, "hi": high, "qx": packed, "bk": came_back, "on": places_out})
        for word in (LAST if last else FLUX).split():
            play(word)
    for sem in SEMAPHORES:
        wait("g", sem, count[sem])
